import numpy as np
import ml_dtypes


def mxq(x, axis, fmt="e4m3"):
    dtype, down = {"e4m3": (ml_dtypes.float8_e4m3fn, 7), "e5m2": (ml_dtypes.float8_e5m2, 14)}[fmt]
    v = np.moveaxis(np.asarray(x, np.float32).astype(ml_dtypes.bfloat16).astype(np.float64), axis, -1)
    blocks = v.reshape(v.shape[:-1] + (-1, 32))
    amax = np.abs(blocks).max(-1, keepdims=True)
    byte = np.maximum(np.where(amax > 0, np.frexp(amax)[1] - 1 + 127, 0) - down, 1)
    scale = np.exp2(byte - 127.0)
    codes = (blocks / scale).astype(np.float32).astype(dtype).astype(np.float64)
    return np.moveaxis((codes * scale).reshape(v.shape), -1, axis)


WIDE = False


def mx_kscale(k):
    if not WIDE:
        return np.ones(k)
    levels = np.array([10, -10, 5, -5, 0])
    if k % 512:
        return np.exp2(np.random.permutation(np.resize(levels, k // 32))).repeat(32)
    a = np.empty((k // 512, 16))
    for p in range(k // 512):
        a[p, :8] = np.random.permutation(np.resize(levels, 8))
        for g in range(8):
            far = levels[np.abs(levels - a[p, g]) >= 10]
            a[p, g + 8] = far[np.random.randint(len(far))]
    return np.exp2(a.ravel()).repeat(32)


BF16 = ml_dtypes.bfloat16


def bf(x):
    return np.asarray(x, np.float32).astype(BF16)


def f64(x):
    return np.asarray(x).astype(np.float64)


E2M1 = np.array([0.0, 0.5, 1.0, 1.5, 2.0, 3.0, 4.0, 6.0, -0.0, -0.5, -1.0, -1.5, -2.0, -3.0, -4.0, -6.0])


def pack_weight(w, fmt):
    k, n = w.shape
    w = f64(bf(w)).reshape(k // 32, 32, n)
    amax = np.abs(w).max(1)
    if fmt == "e4m3":
        byte = np.frexp(amax)[1] - 1 + 127 - 7
    else:
        mant, ex = np.frexp(amax / 6.0)
        byte = np.where(mant > 0.5, ex, ex - 1) + 127
    byte = np.clip(np.where(amax > 0, byte, 1), 1, 254)
    scaled = (w * np.exp2(127.0 - byte)[:, None, :]).reshape(k, n).astype(np.float32)
    by_word = np.ascontiguousarray(scaled.reshape(k // 512, 128, 4, n).transpose(0, 1, 3, 2))
    if fmt == "e4m3":
        words = by_word.astype(ml_dtypes.float8_e4m3fn).view(np.uint8)
    else:
        c = by_word.astype(ml_dtypes.float4_e2m1fn).view(np.uint8) & 0xF
        words = c[..., 0::2] | (c[..., 1::2] << 4)
    return np.ascontiguousarray(words), np.ascontiguousarray(byte.astype(np.uint8).reshape(k // 512, 16, n))


def unpack_weight(words, scales, fmt):
    g, p, n, _ = words.shape
    if fmt == "e4m3":
        vals = np.ascontiguousarray(words).view(ml_dtypes.float8_e4m3fn).astype(np.float64)
    else:
        nib = np.empty((g, p, n, 4), np.uint8)
        nib[..., 0::2] = words & 0xF
        nib[..., 1::2] = words >> 4
        vals = E2M1[nib]
    vals = vals * np.repeat(np.exp2(scales.astype(np.float64) - 127.0), 8, axis=1)[..., None]
    return vals.transpose(0, 1, 3, 2).reshape(g * 512, n)
def pack4(w):
    words, scales = pack_weight(w, "e2m1")
    return words.reshape(words.shape[0], 128, -1), scales


def unpack4(words, scales):
    return unpack_weight(words.reshape(words.shape[0], 128, -1, 2), scales, "e2m1")


T, H, B, D = 1024, 512, 1024, 2048


def setup_inputs():
    s = mx_kscale(B)
    u = mx_kscale(H)
    t = mx_kscale(B)
    a_words, a_scales = pack4(np.random.standard_normal((B, B)) * 0.5 / np.sqrt(B) / s[:, None])
    w_words, w_scales = pack4(np.random.standard_normal((B, D)) / np.sqrt(B) / t[:, None])
    return {"x": bf(np.random.standard_normal((T, B)) * s),
            "a_words": a_words,
            "a_scales": a_scales,
            "c": bf(np.random.standard_normal((T, H)) * 0.5 / np.sqrt(H) / u),
            "y": bf(np.random.standard_normal((H, B)) * u[:, None]),
            "e": bf(np.random.exponential(1.0, (T, B)) * t),
            "w_words": w_words,
            "w_scales": w_scales}


def reference(x, a_words, a_scales, c, y, e, w_words, w_scales):
    a = unpack4(a_words, a_scales)
    w = unpack4(w_words, w_scales)
    across = mxq(f64(x), 1, "e4m3") @ a
    along = mxq(f64(c), 1, "e4m3") @ mxq(f64(y), 0, "e4m3")
    background = across + along
    ratio = f64(e) * np.exp(-background)
    return mxq(ratio, 1, "e4m3") @ w

@@ -1,0 +1,311 @@
+from contextlib import ExitStack
+
+import concourse.mybir as mybir
+from concourse.masks import make_identity
+
+FLOPS = 2 * 1024 * 1024 * 1024 + 2 * 1024 * 512 * 1024 + 2 * 1024 * 1024 * 2048
+
+F32 = mybir.dt.float32
+BF16 = mybir.dt.bfloat16
+I32 = mybir.dt.int32
+U32 = mybir.dt.uint32
+U8 = mybir.dt.uint8
+FP8X4 = mybir.dt.float8_e4m3fn_x4
+FP4X4 = mybir.dt.float4_e2m1fn_x4
+EXP = mybir.ActivationFunctionType.Exp
+MULT = mybir.AluOpType.mult
+
+P = 128
+B, H, D = 1024, 512, 2048
+G = B // 512
+NB = 512
+TILES = 8
+Y_HALF = 512
+Y_V = 352
+
+
+def tile_bearing_time_normaliser_s3_kernel(tc, x, a_words, a_scales, c, y, e, w_words, w_scales, out):
+    nc = tc.nc
+    with ExitStack() as ctx:
+        keep = ctx.enter_context(tc.tile_pool(name="keep", bufs=1))
+        load = ctx.enter_context(tc.tile_pool(name="load", bufs=TILES))
+        work = ctx.enter_context(tc.tile_pool(name="work", bufs=4))
+        psum = ctx.enter_context(tc.psum_pool(name="psum", bufs=1))
+        ctx.enter_context(tc.manual_schedule())
+
+        ident = keep.tile([P, P], F32)
+        a_sb = keep.tile([P, G, 2 * B], U8, align_bytes=64)
+        a_sc = keep.tile([P, G, B], U8, align_bytes=64)
+        w_sb = keep.tile([P, G, 2 * D], U8, align_bytes=64)
+        w_sc = keep.tile([P, G, D], U8, align_bytes=64)
+        y_codes = keep.tile([P, B], U32, align_bytes=64)
+        y_sc = keep.tile([P, B], U8, align_bytes=64)
+        warm_in = keep.tile([P, 8], F32)
+        warm_out = keep.tile([P, 8], F32)
+
+        x_raw, c_raw, e_raw, y_raw = {}, {}, {}, {}
+        x_words, c_words, x_grp, c_grp = {}, {}, {}, {}
+        x_q, c_q, r_q = {}, {}, {}
+        x_ps, c_ps, r_ps = {}, {}, {}
+        l_ps, r_words, r_grp, o_ps, o_sb, y_grp = {}, {}, {}, {}, {}, {}
+
+        def load_x(i):
+            t = load.tile([P, B], BF16, tag="x_raw", name="x_raw")
+            nc.sync.dma_start(out=t[:], in_=x[i * P:(i + 1) * P, :])
+            x_raw[i] = t
+
+        def load_c(i):
+            t = load.tile([P, H], BF16, tag="c_raw", name="c_raw")
+            nc.sync.dma_start(out=t[:], in_=c[i * P:(i + 1) * P, :])
+            c_raw[i] = t
+
+        def load_e(i):
+            t = load.tile([P, B], BF16, tag="e_raw", name="e_raw")
+            nc.sync.dma_start(out=t[:], in_=e[i * P:(i + 1) * P, :])
+            e_raw[i] = t
+
+        def load_y(h):
+            t = keep.tile([P, 4, Y_HALF], BF16, tag="y_raw", name="y_raw", bufs=2)
+            nc.sync.dma_start(out=t[:], in_=y[:, h * Y_HALF:(h + 1) * Y_HALF].rearrange("(p j) n -> p j n", j=4))
+            y_raw[h] = t
+
+        def load_scales(dst, src):
+            for q in range(4):
+                nc.sync.dma_start(
+                    out=dst[32 * q:32 * q + 4, :, :].bitcast(I32),
+                    in_=src[:, 4 * q:4 * q + 4, :].rearrange("g r n -> r g n").bitcast(I32),
+                )
+
+        def permute_x(i):
+            t = work.tile([P, B // 2], F32, tag="x_words", name="x_words")
+            nc.vector.tensor_copy(
+                out=t[:].rearrange("p (g u m) -> p g u m", g=G, u=2),
+                in_=x_raw[i][:].bitcast(F32).rearrange("p (g m u) -> p g u m", g=G, u=2),
+            )
+            x_words[i] = t
+
+        def permute_c(i):
+            t = work.tile([P, H // 2], F32, tag="c_words", name="c_words")
+            nc.vector.tensor_copy(
+                out=t[:].rearrange("p (u m) -> p u m", u=2),
+                in_=c_raw[i][:].bitcast(F32).rearrange("p (m u) -> p u m", u=2),
+            )
+            c_words[i] = t
+
+        def transpose_words(words, count, tag):
+            t = psum.tile([P, count, P], F32, tag=tag, name=tag)
+            for j in range(count):
+                nc.tensor.transpose(t[:, j, :], words[:, j * P:(j + 1) * P], ident[:])
+            return t
+
+        def gather_words(copy, src, passes, tag):
+            t = work.tile([P, passes, P, 4], BF16, tag=tag, name=tag, align_bytes=64)
+            copy(
+                out=t[:].rearrange("p g r j -> p (g r j)").bitcast(F32).rearrange("p (g r u) -> p g r u", g=passes, u=2),
+                in_=src[:].rearrange("p (g u) r -> p g r u", u=2),
+            )
+            return t
+
+        def quantise(grp, passes, tag):
+            codes = work.tile([P, passes * P], U32, tag=tag + "_codes", name=tag + "_codes", align_bytes=64)
+            scales = work.tile([P, passes * P], U8, tag=tag + "_sc", name=tag + "_sc", align_bytes=64)
+            nc.vector.quantize_mx(
+                out=codes[:].bitcast(FP8X4), scales=scales[:], in_=grp[:].rearrange("p g r j -> p (g r j)"))
+            return codes, scales
+
+        def y_interleave(h):
+            t = keep.tile([P, Y_HALF, 4], BF16, tag="y_grp", name="y_grp", bufs=2, align_bytes=64)
+            nc.vector.tensor_copy(out=t[:, :Y_V, :], in_=y_raw[h][:, :, :Y_V].rearrange("p j n -> p n j"))
+            nc.scalar.copy(out=t[:, Y_V:, :], in_=y_raw[h][:, :, Y_V:].rearrange("p j n -> p n j"))
+            y_grp[h] = t
+
+        def y_quantise(h):
+            cols = slice(h * Y_HALF, (h + 1) * Y_HALF)
+            nc.vector.quantize_mx(
+                out=y_codes[:, cols].bitcast(FP8X4), scales=y_sc[:, cols], in_=y_grp[h][:].rearrange("p n j -> p (n j)"))
+
+        def mm_xa(i):
+            codes, scales = x_q[i]
+            for n in range(2):
+                t = psum.tile([P, NB], F32, tag="acc", name="acc", bufs=5)
+                for g in range(G):
+                    nc.tensor.matmul_mx(
+                        out=t[:],
+                        lhsT=codes[:, g * P:(g + 1) * P].bitcast(FP8X4),
+                        lhsT_scale=scales[:, g * P:(g + 1) * P],
+                        rhs=a_sb[:, g, 2 * NB * n:2 * NB * (n + 1)].bitcast(FP4X4),
+                        rhs_scale=a_sc[:, g, NB * n:NB * (n + 1)],
+                        start=(g == 0),
+                        stop=False,
+                    )
+                l_ps[i, n] = t
+
+        def mm_cy(i):
+            codes, scales = c_q[i]
+            for n in range(2):
+                nc.tensor.matmul_mx(
+                    out=l_ps[i, n][:],
+                    lhsT=codes[:].bitcast(FP8X4),
+                    lhsT_scale=scales[:],
+                    rhs=y_codes[:, NB * n:NB * (n + 1)].bitcast(FP8X4),
+                    rhs_scale=y_sc[:, NB * n:NB * (n + 1)],
+                    start=False,
+                    stop=True,
+                )
+
+        def mm_layer1(i):
+            codes, scales = x_q[i]
+            c_codes, c_scales = c_q[i]
+            for n in range(2):
+                t = psum.tile([P, NB], F32, tag="acc", name="acc", bufs=5)
+                for g in range(G):
+                    nc.tensor.matmul_mx(
+                        out=t[:],
+                        lhsT=codes[:, g * P:(g + 1) * P].bitcast(FP8X4),
+                        lhsT_scale=scales[:, g * P:(g + 1) * P],
+                        rhs=a_sb[:, g, 2 * NB * n:2 * NB * (n + 1)].bitcast(FP4X4),
+                        rhs_scale=a_sc[:, g, NB * n:NB * (n + 1)],
+                        start=(g == 0),
+                        stop=False,
+                    )
+                nc.tensor.matmul_mx(
+                    out=t[:],
+                    lhsT=c_codes[:].bitcast(FP8X4),
+                    lhsT_scale=c_scales[:],
+                    rhs=y_codes[:, NB * n:NB * (n + 1)].bitcast(FP8X4),
+                    rhs_scale=y_sc[:, NB * n:NB * (n + 1)],
+                    start=False,
+                    stop=True,
+                )
+                l_ps[i, n] = t
+
+        def exp_and_multiply(i):
+            r = work.tile([P, B], BF16, tag="r_words", name="r_words")
+            for n in range(2):
+                t = work.tile([P, NB], F32, tag="inv_bg", name="inv_bg")
+                nc.scalar.activation(out=t[:], in_=l_ps[i, n][:], func=EXP, scale=-1.0)
+                cols = slice(n * NB, (n + 1) * NB)
+                nc.vector.tensor_tensor(
+                    out=r[:, cols].rearrange("p (u m h) -> p u m h", u=2, h=2),
+                    in0=t[:].rearrange("p (m u h) -> p u m h", u=2, h=2),
+                    in1=e_raw[i][:, cols].rearrange("p (m u h) -> p u m h", u=2, h=2),
+                    op=MULT,
+                )
+            r_words[i] = r
+
+        def mm_layer2(i, n):
+            codes, scales = r_q[i]
+            t = psum.tile([P, NB], F32, tag="acc", name="acc", bufs=5)
+            for g in range(G):
+                nc.tensor.matmul_mx(
+                    out=t[:],
+                    lhsT=codes[:, g * P:(g + 1) * P].bitcast(FP8X4),
+                    lhsT_scale=scales[:, g * P:(g + 1) * P],
+                    rhs=w_sb[:, g, 2 * NB * n:2 * NB * (n + 1)].bitcast(FP4X4),
+                    rhs_scale=w_sc[:, g, NB * n:NB * (n + 1)],
+                    start=(g == 0),
+                    stop=(g == G - 1),
+                )
+            o_ps[i, n] = t
+
+        def copy_out(i, n):
+            if n == 0:
+                o = work.tile([P, D], F32, tag="o_sb", name="o_sb")
+                o_sb[i] = o
+            copy = nc.scalar.copy if n % 2 == 0 else nc.vector.tensor_copy
+            copy(out=o_sb[i][:, n * NB:(n + 1) * NB], in_=o_ps[i, n][:])
+            if n % 2 == 1:
+                cols = slice((n - 1) * NB, (n + 1) * NB)
+                nc.sync.dma_start(out=out[i * P:(i + 1) * P, cols], in_=o_sb[i][:, cols])
+
+        nc.vector.memset(a_sc[:].rearrange("p g n -> p (g n)").bitcast(I32), 0)
+        nc.vector.memset(w_sc[:].rearrange("p g n -> p (g n)").bitcast(I32), 0)
+        nc.vector.memset(warm_in[:], 0.0)
+        make_identity(nc, ident[:])
+        nc.scalar.activation(out=warm_out[:], in_=warm_in[:], func=EXP, scale=-1.0)
+
+        load_x(0)
+        load_scales(a_sc, a_scales)
+        for g in range(G):
+            nc.sync.dma_start(out=a_sb[:, g, :].bitcast(I32), in_=a_words[g].bitcast(I32))
+        load_c(0)
+        load_x(1)
+        load_y(0)
+        load_y(1)
+        load_c(1)
+        load_e(0)
+        load_x(2)
+        load_c(2)
+        load_scales(w_sc, w_scales)
+        for h in range(2):
+            cols = slice(h * D, (h + 1) * D)
+            nc.sync.dma_start(
+                out=w_sb[:, :, cols].bitcast(I32),
+                in_=w_words[:, :, cols].rearrange("g p n -> p g n").bitcast(I32))
+        load_e(1)
+        for i in range(3, TILES):
+            load_x(i)
+            load_c(i)
+            load_e(i - 1)
+        load_e(TILES - 1)
+
+        permute_x(0)
+        x_ps[0] = transpose_words(x_words[0], 4, "xt")
+        x_grp[0] = gather_words(nc.scalar.copy, x_ps[0], 2, "x_grp")
+        permute_c(0)
+        permute_x(1)
+        x_q[0] = quantise(x_grp[0], 2, "x")
+        c_ps[0] = transpose_words(c_words[0], 2, "ct")
+        c_grp[0] = gather_words(nc.scalar.copy, c_ps[0], 1, "c_grp")
+        x_ps[1] = transpose_words(x_words[1], 4, "xt")
+        x_grp[1] = gather_words(nc.scalar.copy, x_ps[1], 2, "x_grp")
+        mm_xa(0)
+        y_interleave(0)
+        c_q[0] = quantise(c_grp[0], 1, "c")
+        x_q[1] = quantise(x_grp[1], 2, "x")
+        mm_xa(1)
+        y_quantise(0)
+        y_interleave(1)
+        permute_c(1)
+        y_quantise(1)
+        c_ps[1] = transpose_words(c_words[1], 2, "ct")
+        c_grp[1] = gather_words(nc.scalar.copy, c_ps[1], 1, "c_grp")
+        permute_x(2)
+        c_q[1] = quantise(c_grp[1], 1, "c")
+        permute_c(2)
+        mm_cy(0)
+        exp_and_multiply(0)
+        mm_cy(1)
+        x_ps[2] = transpose_words(x_words[2], 4, "xt")
+        x_grp[2] = gather_words(nc.scalar.copy, x_ps[2], 2, "x_grp")
+        c_ps[2] = transpose_words(c_words[2], 2, "ct")
+        c_grp[2] = gather_words(nc.scalar.copy, c_ps[2], 1, "c_grp")
+        exp_and_multiply(1)
+        x_q[2] = quantise(x_grp[2], 2, "x")
+        c_q[2] = quantise(c_grp[2], 1, "c")
+        permute_x(3)
+        permute_c(3)
+
+        for i in range(TILES):
+            new, ahead = i + 3, i + 2
+            r_ps[i] = transpose_words(r_words[i][:].bitcast(F32), 4, "rt")
+            if new < TILES:
+                x_ps[new] = transpose_words(x_words[new], 4, "xt")
+                c_ps[new] = transpose_words(c_words[new], 2, "ct")
+            r_grp[i] = gather_words(nc.vector.tensor_copy, r_ps[i], 2, "r_grp")
+            if new < TILES:
+                x_grp[new] = gather_words(nc.scalar.copy, x_ps[new], 2, "x_grp")
+                c_grp[new] = gather_words(nc.scalar.copy, c_ps[new], 1, "c_grp")
+            if new + 1 < TILES:
+                permute_x(new + 1)
+                permute_c(new + 1)
+            r_q[i] = quantise(r_grp[i], 2, "r")
+            if new < TILES:
+                x_q[new] = quantise(x_grp[new], 2, "x")
+                c_q[new] = quantise(c_grp[new], 1, "c")
+            if ahead < TILES:
+                mm_layer1(ahead)
+                exp_and_multiply(ahead)
+            for n in range(4):
+                mm_layer2(i, n)
+                copy_out(i, n)

@@ -36,7 +36,7 @@ def tile_bearing_time_normaliser_s3_kernel(tc, x, a_words, a_scales, c, y, e, w_
         ident = keep.tile([P, P], F32)
         a_sb = keep.tile([P, G, 2 * B], U8, align_bytes=64)
         a_sc = keep.tile([P, G, B], U8, align_bytes=64)
-        w_sb = keep.tile([P, G, 2 * D], U8, align_bytes=64)
+        w_sb = [keep.tile([P, G, D], U8, tag="w_sb", name="w_sb", bufs=2, align_bytes=64) for h in range(2)]
         w_sc = keep.tile([P, G, D], U8, align_bytes=64)
         y_codes = keep.tile([P, B], U32, align_bytes=64)
         y_sc = keep.tile([P, B], U8, align_bytes=64)
@@ -47,7 +47,7 @@ def tile_bearing_time_normaliser_s3_kernel(tc, x, a_words, a_scales, c, y, e, w_
         x_words, c_words, x_grp, c_grp = {}, {}, {}, {}
         x_q, c_q, r_q = {}, {}, {}
         x_ps, c_ps, r_ps = {}, {}, {}
-        l_ps, r_words, r_grp, o_ps, o_sb, y_grp = {}, {}, {}, {}, {}, {}
+        l_ps, inv_bg, r_words, r_grp, o_ps, o_sb, y_grp = {}, {}, {}, {}, {}, {}, {}
 
         def load_x(i):
             t = load.tile([P, B], BF16, tag="x_raw", name="x_raw")
@@ -69,24 +69,24 @@ def tile_bearing_time_normaliser_s3_kernel(tc, x, a_words, a_scales, c, y, e, w_
             nc.sync.dma_start(out=t[:], in_=y[:, h * Y_HALF:(h + 1) * Y_HALF].rearrange("(p j) n -> p j n", j=4))
             y_raw[h] = t
 
-        def load_scales(dst, src):
+        def load_scales(queue, dst, src):
             for q in range(4):
-                nc.sync.dma_start(
+                queue.dma_start(
                     out=dst[32 * q:32 * q + 4, :, :].bitcast(I32),
                     in_=src[:, 4 * q:4 * q + 4, :].rearrange("g r n -> r g n").bitcast(I32),
                 )
 
-        def permute_x(i):
+        def permute_x(i, copy=nc.scalar.copy):
             t = work.tile([P, B // 2], F32, tag="x_words", name="x_words")
-            nc.vector.tensor_copy(
+            copy(
                 out=t[:].rearrange("p (g u m) -> p g u m", g=G, u=2),
                 in_=x_raw[i][:].bitcast(F32).rearrange("p (g m u) -> p g u m", g=G, u=2),
             )
             x_words[i] = t
 
-        def permute_c(i):
+        def permute_c(i, copy=nc.scalar.copy):
             t = work.tile([P, H // 2], F32, tag="c_words", name="c_words")
-            nc.vector.tensor_copy(
+            copy(
                 out=t[:].rearrange("p (u m) -> p u m", u=2),
                 in_=c_raw[i][:].bitcast(F32).rearrange("p (m u) -> p u m", u=2),
             )
@@ -179,19 +179,22 @@ def tile_bearing_time_normaliser_s3_kernel(tc, x, a_words, a_scales, c, y, e, w_
                 )
                 l_ps[i, n] = t
 
-        def exp_and_multiply(i):
-            r = work.tile([P, B], BF16, tag="r_words", name="r_words")
-            for n in range(2):
-                t = work.tile([P, NB], F32, tag="inv_bg", name="inv_bg")
-                nc.scalar.activation(out=t[:], in_=l_ps[i, n][:], func=EXP, scale=-1.0)
-                cols = slice(n * NB, (n + 1) * NB)
-                nc.vector.tensor_tensor(
-                    out=r[:, cols].rearrange("p (u m h) -> p u m h", u=2, h=2),
-                    in0=t[:].rearrange("p (m u h) -> p u m h", u=2, h=2),
-                    in1=e_raw[i][:, cols].rearrange("p (m u h) -> p u m h", u=2, h=2),
-                    op=MULT,
-                )
-            r_words[i] = r
+        def inverse_background(i, n):
+            t = work.tile([P, NB], F32, tag="inv_bg", name="inv_bg", bufs=6)
+            nc.scalar.activation(out=t[:], in_=l_ps[i, n][:], func=EXP, scale=-1.0)
+            inv_bg[i, n] = t
+
+        def multiply(i, n):
+            if n == 0:
+                r = work.tile([P, B], BF16, tag="r_words", name="r_words")
+                r_words[i] = r
+            cols = slice(n * NB, (n + 1) * NB)
+            nc.vector.tensor_tensor(
+                out=r_words[i][:, cols].rearrange("p (u m h) -> p u m h", u=2, h=2),
+                in0=inv_bg[i, n][:].rearrange("p (m u h) -> p u m h", u=2, h=2),
+                in1=e_raw[i][:, cols].rearrange("p (m u h) -> p u m h", u=2, h=2),
+                op=MULT,
+            )
 
         def mm_layer2(i, n):
             codes, scales = r_q[i]
@@ -201,111 +204,271 @@ def tile_bearing_time_normaliser_s3_kernel(tc, x, a_words, a_scales, c, y, e, w_
                     out=t[:],
                     lhsT=codes[:, g * P:(g + 1) * P].bitcast(FP8X4),
                     lhsT_scale=scales[:, g * P:(g + 1) * P],
-                    rhs=w_sb[:, g, 2 * NB * n:2 * NB * (n + 1)].bitcast(FP4X4),
+                    rhs=w_sb[n // 2][:, g, 2 * NB * (n % 2):2 * NB * (n % 2 + 1)].bitcast(FP4X4),
                     rhs_scale=w_sc[:, g, NB * n:NB * (n + 1)],
                     start=(g == 0),
                     stop=(g == G - 1),
                 )
             o_ps[i, n] = t
 
+        def store(i, lo, hi):
+            nc.sync.dma_start(out=out[i * P:(i + 1) * P, lo:hi], in_=o_sb[i][:, lo:hi])
+
         def copy_out(i, n):
             if n == 0:
                 o = work.tile([P, D], F32, tag="o_sb", name="o_sb")
                 o_sb[i] = o
+            lo, mid, hi = n * NB, n * NB + NB // 2, (n + 1) * NB
+            if (i, n) == (TILES - 1, 3):
+                nc.scalar.copy(out=o_sb[i][:, lo:mid], in_=o_ps[i, n][:, :NB // 2])
+                store(i, lo, mid)
+                nc.vector.tensor_copy(out=o_sb[i][:, mid:hi], in_=o_ps[i, n][:, NB // 2:])
+                store(i, mid, hi)
+                return
             copy = nc.scalar.copy if n % 2 == 0 else nc.vector.tensor_copy
-            copy(out=o_sb[i][:, n * NB:(n + 1) * NB], in_=o_ps[i, n][:])
-            if n % 2 == 1:
-                cols = slice((n - 1) * NB, (n + 1) * NB)
-                nc.sync.dma_start(out=out[i * P:(i + 1) * P, cols], in_=o_sb[i][:, cols])
+            copy(out=o_sb[i][:, lo:hi], in_=o_ps[i, n][:])
+            if i == TILES - 1:
+                store(i, lo, hi)
+            elif n % 2 == 1:
+                store(i, lo - NB, hi)
 
         nc.vector.memset(a_sc[:].rearrange("p g n -> p (g n)").bitcast(I32), 0)
-        nc.vector.memset(w_sc[:].rearrange("p g n -> p (g n)").bitcast(I32), 0)
         nc.vector.memset(warm_in[:], 0.0)
+        nc.vector.memset(w_sc[:].rearrange("p g n -> p (g n)").bitcast(I32), 0)
         make_identity(nc, ident[:])
         nc.scalar.activation(out=warm_out[:], in_=warm_in[:], func=EXP, scale=-1.0)
 
-        load_x(0)
-        load_scales(a_sc, a_scales)
-        for g in range(G):
-            nc.sync.dma_start(out=a_sb[:, g, :].bitcast(I32), in_=a_words[g].bitcast(I32))
-        load_c(0)
-        load_x(1)
-        load_y(0)
-        load_y(1)
-        load_c(1)
-        load_e(0)
-        load_x(2)
-        load_c(2)
-        load_scales(w_sc, w_scales)
-        for h in range(2):
-            cols = slice(h * D, (h + 1) * D)
+        def load_w(h):
             nc.sync.dma_start(
-                out=w_sb[:, :, cols].bitcast(I32),
-                in_=w_words[:, :, cols].rearrange("g p n -> p g n").bitcast(I32))
-        load_e(1)
-        for i in range(3, TILES):
-            load_x(i)
-            load_c(i)
-            load_e(i - 1)
-        load_e(TILES - 1)
+                out=w_sb[h][:].bitcast(I32),
+                in_=w_words[:, :, h * D:(h + 1) * D].rearrange("g p n -> p g n").bitcast(I32))
 
-        permute_x(0)
-        x_ps[0] = transpose_words(x_words[0], 4, "xt")
-        x_grp[0] = gather_words(nc.scalar.copy, x_ps[0], 2, "x_grp")
-        permute_c(0)
-        permute_x(1)
-        x_q[0] = quantise(x_grp[0], 2, "x")
-        c_ps[0] = transpose_words(c_words[0], 2, "ct")
-        c_grp[0] = gather_words(nc.scalar.copy, c_ps[0], 1, "c_grp")
-        x_ps[1] = transpose_words(x_words[1], 4, "xt")
-        x_grp[1] = gather_words(nc.scalar.copy, x_ps[1], 2, "x_grp")
-        mm_xa(0)
-        y_interleave(0)
-        c_q[0] = quantise(c_grp[0], 1, "c")
-        x_q[1] = quantise(x_grp[1], 2, "x")
-        mm_xa(1)
-        y_quantise(0)
-        y_interleave(1)
-        permute_c(1)
-        y_quantise(1)
-        c_ps[1] = transpose_words(c_words[1], 2, "ct")
-        c_grp[1] = gather_words(nc.scalar.copy, c_ps[1], 1, "c_grp")
-        permute_x(2)
-        c_q[1] = quantise(c_grp[1], 1, "c")
-        permute_c(2)
-        mm_cy(0)
-        exp_and_multiply(0)
-        mm_cy(1)
-        x_ps[2] = transpose_words(x_words[2], 4, "xt")
-        x_grp[2] = gather_words(nc.scalar.copy, x_ps[2], 2, "x_grp")
-        c_ps[2] = transpose_words(c_words[2], 2, "ct")
-        c_grp[2] = gather_words(nc.scalar.copy, c_ps[2], 1, "c_grp")
-        exp_and_multiply(1)
-        x_q[2] = quantise(x_grp[2], 2, "x")
-        c_q[2] = quantise(c_grp[2], 1, "c")
-        permute_x(3)
-        permute_c(3)
+        def transpose_x(i, tag="xt"):
+            x_ps[i] = transpose_words(x_words[i], 4, tag)
 
-        for i in range(TILES):
-            new, ahead = i + 3, i + 2
-            r_ps[i] = transpose_words(r_words[i][:].bitcast(F32), 4, "rt")
-            if new < TILES:
-                x_ps[new] = transpose_words(x_words[new], 4, "xt")
-                c_ps[new] = transpose_words(c_words[new], 2, "ct")
+        def transpose_c(i, tag="ct"):
+            c_ps[i] = transpose_words(c_words[i], 2, tag)
+
+        def gather_x(i, copy=nc.scalar.copy):
+            x_grp[i] = gather_words(copy, x_ps[i], 2, "x_grp")
+
+        def gather_c(i, copy=nc.scalar.copy):
+            c_grp[i] = gather_words(copy, c_ps[i], 1, "c_grp")
+
+        def quantise_x(i):
+            x_q[i] = quantise(x_grp[i], 2, "x")
+
+        def quantise_c(i):
+            c_q[i] = quantise(c_grp[i], 1, "c")
+
+        def transpose_r(i):
+            tag = "xt" if i == TILES - 2 else "rt"
+            r_ps[i] = transpose_words(r_words[i][:].bitcast(F32), 4, tag)
+
+        def gather_r(i):
             r_grp[i] = gather_words(nc.vector.tensor_copy, r_ps[i], 2, "r_grp")
-            if new < TILES:
-                x_grp[new] = gather_words(nc.scalar.copy, x_ps[new], 2, "x_grp")
-                c_grp[new] = gather_words(nc.scalar.copy, c_ps[new], 1, "c_grp")
-            if new + 1 < TILES:
-                permute_x(new + 1)
-                permute_c(new + 1)
+
+        def quantise_r(i):
             r_q[i] = quantise(r_grp[i], 2, "r")
-            if new < TILES:
-                x_q[new] = quantise(x_grp[new], 2, "x")
-                c_q[new] = quantise(c_grp[new], 1, "c")
-            if ahead < TILES:
-                mm_layer1(ahead)
-                exp_and_multiply(ahead)
-            for n in range(4):
-                mm_layer2(i, n)
-                copy_out(i, n)
+
+        def layer2(i, n):
+            mm_layer2(i, n)
+            copy_out(i, n)
+
+        vcopy = nc.vector.tensor_copy
+        load_c(0)
+        load_x(0)
+        load_y(0)
+        load_scales(nc.sync, a_sc, a_scales)
+        load_y(1)
+        nc.sync.dma_start(out=a_sb[:].bitcast(I32), in_=a_words.rearrange("g p n -> p g n").bitcast(I32))
+        load_x(1)
+        load_c(1)
+        load_x(3)
+        load_x(2)
+        load_c(4)
+        load_c(2)
+        load_x(4)
+        load_e(2)
+        load_c(3)
+        load_scales(nc.gpsimd, w_sc, w_scales)
+        load_e(0)
+        load_e(1)
+        load_w(0)
+        load_w(1)
+        load_e(3)
+        load_x(5)
+        load_c(5)
+        load_e(4)
+        load_x(6)
+        load_c(6)
+        load_e(5)
+        load_x(7)
+        load_c(7)
+        load_e(6)
+        load_e(7)
+        permute_c(0, vcopy)
+        permute_x(0, vcopy)
+        transpose_x(0)
+        gather_x(0)
+        y_interleave(0)
+        transpose_c(0)
+        quantise_x(0)
+        y_interleave(1)
+        mm_xa(0)
+        permute_x(1, vcopy)
+        y_quantise(0)
+        permute_c(1, vcopy)
+        transpose_x(1)
+        gather_c(0)
+        quantise_c(0)
+        y_quantise(1)
+        permute_x(2, vcopy)
+        transpose_c(1)
+        mm_cy(0)
+        transpose_x(2)
+        permute_c(2, vcopy)
+        gather_x(1)
+        gather_c(1)
+        transpose_c(2)
+        quantise_x(1)
+        permute_x(3, vcopy)
+        inverse_background(0, 0)
+        quantise_c(1)
+        gather_c(2)
+        permute_c(3, vcopy)
+        multiply(0, 0)
+        mm_layer1(1)
+        transpose_c(3)
+        quantise_c(2)
+        inverse_background(0, 1)
+        gather_x(2)
+        inverse_background(1, 0)
+        transpose_x(3)
+        gather_x(3)
+        multiply(0, 1)
+        gather_c(3)
+        quantise_x(2)
+        inverse_background(1, 1)
+        transpose_r(0)
+        multiply(1, 0)
+        mm_layer1(2)
+        gather_r(0)
+        inverse_background(2, 0)
+        inverse_background(2, 1)
+        quantise_x(3)
+        quantise_r(0)
+        layer2(0, 0)
+        multiply(1, 1)
+        quantise_c(3)
+        multiply(2, 0)
+        multiply(2, 1)
+        permute_c(4)
+        permute_x(4)
+        layer2(0, 1)
+        layer2(0, 2)
+        layer2(0, 3)
+        transpose_r(1)
+        transpose_x(4)
+        transpose_c(4)
+        gather_r(1)
+        gather_x(4)
+        gather_c(4)
+        quantise_r(1)
+        quantise_x(4)
+        quantise_c(4)
+        mm_layer1(3)
+        inverse_background(3, 0)
+        permute_c(5)
+        inverse_background(3, 1)
+        multiply(3, 0)
+        multiply(3, 1)
+        layer2(1, 0)
+        permute_x(5)
+        layer2(1, 1)
+        layer2(1, 2)
+        layer2(1, 3)
+        transpose_r(2)
+        transpose_x(5)
+        transpose_c(5)
+        gather_r(2)
+        gather_x(5)
+        gather_c(5)
+        quantise_r(2)
+        quantise_x(5)
+        quantise_c(5)
+        mm_layer1(4)
+        inverse_background(4, 0)
+        permute_c(6)
+        inverse_background(4, 1)
+        multiply(4, 0)
+        multiply(4, 1)
+        layer2(2, 0)
+        permute_x(6)
+        layer2(2, 1)
+        layer2(2, 2)
+        layer2(2, 3)
+        transpose_r(3)
+        transpose_x(6)
+        transpose_c(6)
+        gather_r(3)
+        gather_x(6)
+        gather_c(6)
+        quantise_r(3)
+        quantise_x(6)
+        quantise_c(6)
+        mm_layer1(5)
+        inverse_background(5, 0)
+        permute_c(7)
+        inverse_background(5, 1)
+        multiply(5, 0)
+        multiply(5, 1)
+        layer2(3, 0)
+        permute_x(7)
+        layer2(3, 1)
+        layer2(3, 2)
+        layer2(3, 3)
+        transpose_r(4)
+        transpose_x(7)
+        transpose_c(7)
+        gather_r(4)
+        gather_x(7)
+        gather_c(7)
+        quantise_r(4)
+        quantise_x(7)
+        quantise_c(7)
+        mm_layer1(6)
+        inverse_background(6, 0)
+        inverse_background(6, 1)
+        multiply(6, 0)
+        multiply(6, 1)
+        layer2(4, 0)
+        layer2(4, 1)
+        layer2(4, 2)
+        layer2(4, 3)
+        transpose_r(5)
+        transpose_r(6)
+        gather_r(5)
+        gather_r(6)
+        quantise_r(5)
+        quantise_r(6)
+        mm_layer1(7)
+        inverse_background(7, 0)
+        inverse_background(7, 1)
+        multiply(7, 0)
+        multiply(7, 1)
+        layer2(5, 0)
+        layer2(5, 1)
+        layer2(5, 2)
+        layer2(5, 3)
+        transpose_r(7)
+        gather_r(7)
+        quantise_r(7)
+        layer2(6, 0)
+        layer2(6, 1)
+        layer2(6, 2)
+        layer2(6, 3)
+        layer2(7, 0)
+        layer2(7, 1)
+        layer2(7, 2)
+        layer2(7, 3)

@@ -16,11 +16,11 @@ EXP = mybir.ActivationFunctionType.Exp
 MULT = mybir.AluOpType.mult
 
 P = 128
+TILES = 8
 B, H, D = 1024, 512, 2048
 G = B // 512
 NB = 512
-TILES = 8
-Y_HALF = 512
+BANKS = 8
 Y_V = 352
 
 
@@ -28,9 +28,8 @@ def tile_bearing_time_normaliser_s3_kernel(tc, x, a_words, a_scales, c, y, e, w_
     nc = tc.nc
     with ExitStack() as ctx:
         keep = ctx.enter_context(tc.tile_pool(name="keep", bufs=1))
-        load = ctx.enter_context(tc.tile_pool(name="load", bufs=TILES))
-        work = ctx.enter_context(tc.tile_pool(name="work", bufs=4))
-        psum = ctx.enter_context(tc.psum_pool(name="psum", bufs=1))
+        work = ctx.enter_context(tc.tile_pool(name="work", bufs=5))
+        psum = ctx.enter_context(tc.psum_pool(name="psum", bufs=BANKS))
         ctx.enter_context(tc.manual_schedule())
 
         ident = keep.tile([P, P], F32)
@@ -38,156 +37,156 @@ def tile_bearing_time_normaliser_s3_kernel(tc, x, a_words, a_scales, c, y, e, w_
         a_sc = keep.tile([P, G, B], U8, align_bytes=64)
         w_sb = [keep.tile([P, G, D], U8, tag="w_sb", name="w_sb", bufs=2, align_bytes=64) for h in range(2)]
         w_sc = keep.tile([P, G, D], U8, align_bytes=64)
+        y_raw = keep.tile([P, 4, B], BF16)
         y_codes = keep.tile([P, B], U32, align_bytes=64)
         y_sc = keep.tile([P, B], U8, align_bytes=64)
         warm_in = keep.tile([P, 8], F32)
         warm_out = keep.tile([P, 8], F32)
 
-        x_raw, c_raw, e_raw, y_raw = {}, {}, {}, {}
-        x_words, c_words, x_grp, c_grp = {}, {}, {}, {}
+        x_raw, c_raw, e_raw = {}, {}, {}
+        x_words, c_words, r_words = {}, {}, {}
+        x_ps, c_ps, r_ps, l_ps, o_ps = {}, {}, {}, {}, {}
+        x_grp, c_grp, r_grp, y_grp = {}, {}, {}, {}
         x_q, c_q, r_q = {}, {}, {}
-        x_ps, c_ps, r_ps = {}, {}, {}
-        l_ps, inv_bg, r_words, r_grp, o_ps, o_sb, y_grp = {}, {}, {}, {}, {}, {}, {}
+        inv_bg, o_sb = {}, {}
 
-        def load_x(i):
-            t = load.tile([P, B], BF16, tag="x_raw", name="x_raw")
-            nc.sync.dma_start(out=t[:], in_=x[i * P:(i + 1) * P, :])
-            x_raw[i] = t
+        out_rows = out.rearrange("(p i) d -> p i d", i=TILES)
 
-        def load_c(i):
-            t = load.tile([P, H], BF16, tag="c_raw", name="c_raw")
-            nc.sync.dma_start(out=t[:], in_=c[i * P:(i + 1) * P, :])
-            c_raw[i] = t
+        def load_rows(src, raw, tag, lo, hi):
+            rows = src.rearrange("(p i) b -> p i b", i=TILES)
+            t = keep.tile([P, hi - lo, rows.shape[2]], BF16, tag=tag + str(lo), name=tag + str(lo))
+            nc.sync.dma_start(out=t[:], in_=rows[:, lo:hi, :])
+            for i in range(lo, hi):
+                raw[i] = t[:, i - lo, :]
 
-        def load_e(i):
-            t = load.tile([P, B], BF16, tag="e_raw", name="e_raw")
-            nc.sync.dma_start(out=t[:], in_=e[i * P:(i + 1) * P, :])
-            e_raw[i] = t
-
-        def load_y(h):
-            t = keep.tile([P, 4, Y_HALF], BF16, tag="y_raw", name="y_raw", bufs=2)
-            nc.sync.dma_start(out=t[:], in_=y[:, h * Y_HALF:(h + 1) * Y_HALF].rearrange("(p j) n -> p j n", j=4))
-            y_raw[h] = t
-
-        def load_scales(queue, dst, src):
+        def load_scales(dst, src):
             for q in range(4):
-                queue.dma_start(
+                nc.sync.dma_start(
                     out=dst[32 * q:32 * q + 4, :, :].bitcast(I32),
                     in_=src[:, 4 * q:4 * q + 4, :].rearrange("g r n -> r g n").bitcast(I32),
                 )
 
-        def permute_x(i, copy=nc.scalar.copy):
-            t = work.tile([P, B // 2], F32, tag="x_words", name="x_words")
-            copy(
-                out=t[:].rearrange("p (g u m) -> p g u m", g=G, u=2),
-                in_=x_raw[i][:].bitcast(F32).rearrange("p (g m u) -> p g u m", g=G, u=2),
-            )
-            x_words[i] = t
+        def load_w(h):
+            nc.sync.dma_start(
+                out=w_sb[h][:].bitcast(I32),
+                in_=w_words[:, :, h * D:(h + 1) * D].rearrange("g p n -> p g n").bitcast(I32))
 
-        def permute_c(i, copy=nc.scalar.copy):
-            t = work.tile([P, H // 2], F32, tag="c_words", name="c_words")
+        def order_words(copy, raw, passes, tag):
+            t = work.tile([P, passes * 256], F32, tag=tag, name=tag)
             copy(
-                out=t[:].rearrange("p (u m) -> p u m", u=2),
-                in_=c_raw[i][:].bitcast(F32).rearrange("p (m u) -> p u m", u=2),
+                out=t[:].rearrange("p (g u m) -> p g u m", g=passes, u=2),
+                in_=raw.bitcast(F32).rearrange("p (g m u) -> p g u m", g=passes, u=2),
             )
-            c_words[i] = t
-
-        def transpose_words(words, count, tag):
-            t = psum.tile([P, count, P], F32, tag=tag, name=tag)
-            for j in range(count):
-                nc.tensor.transpose(t[:, j, :], words[:, j * P:(j + 1) * P], ident[:])
             return t
 
-        def gather_words(copy, src, passes, tag):
+        def new_bank():
+            t = psum.tile([P, NB], F32, tag="bank", name="bank")
+            return t
+
+        def transpose_words(words, count):
+            t = new_bank()
+            for j in range(count):
+                nc.tensor.transpose(t[:, j * P:(j + 1) * P], words[:, j * P:(j + 1) * P], ident[:])
+            return t
+
+        def interleave(copy, bank, passes, tag):
             t = work.tile([P, passes, P, 4], BF16, tag=tag, name=tag, align_bytes=64)
             copy(
-                out=t[:].rearrange("p g r j -> p (g r j)").bitcast(F32).rearrange("p (g r u) -> p g r u", g=passes, u=2),
-                in_=src[:].rearrange("p (g u) r -> p g r u", u=2),
+                out=t[:].rearrange("p g r t -> p (g r t)").bitcast(F32).rearrange("p (g r u) -> p g r u", g=passes, u=2),
+                in_=bank[:, :passes * 2 * P].rearrange("p (g u r) -> p g r u", g=passes, u=2),
             )
             return t
 
         def quantise(grp, passes, tag):
-            codes = work.tile([P, passes * P], U32, tag=tag + "_codes", name=tag + "_codes", align_bytes=64)
-            scales = work.tile([P, passes * P], U8, tag=tag + "_sc", name=tag + "_sc", align_bytes=64)
+            codes = work.tile([P, passes * P], U32, tag=tag + "_codes", name=tag + "_codes", bufs=TILES, align_bytes=64)
+            scales = work.tile([P, passes * P], U8, tag=tag + "_sc", name=tag + "_sc", bufs=TILES, align_bytes=64)
             nc.vector.quantize_mx(
-                out=codes[:].bitcast(FP8X4), scales=scales[:], in_=grp[:].rearrange("p g r j -> p (g r j)"))
+                out=codes[:].bitcast(FP8X4), scales=scales[:], in_=grp[:].rearrange("p g r t -> p (g r t)"))
             return codes, scales
 
-        def y_interleave(h):
-            t = keep.tile([P, Y_HALF, 4], BF16, tag="y_grp", name="y_grp", bufs=2, align_bytes=64)
-            nc.vector.tensor_copy(out=t[:, :Y_V, :], in_=y_raw[h][:, :, :Y_V].rearrange("p j n -> p n j"))
-            nc.scalar.copy(out=t[:, Y_V:, :], in_=y_raw[h][:, :, Y_V:].rearrange("p j n -> p n j"))
-            y_grp[h] = t
+        def mx_pass(bank, operand, g, codes, code_type, scales, start, stop):
+            nc.tensor.matmul_mx(
+                out=bank[:],
+                lhsT=operand[0][:, g * P:(g + 1) * P].bitcast(FP8X4),
+                lhsT_scale=operand[1][:, g * P:(g + 1) * P],
+                rhs=codes.bitcast(code_type),
+                rhs_scale=scales,
+                start=start,
+                stop=stop,
+            )
 
-        def y_quantise(h):
-            cols = slice(h * Y_HALF, (h + 1) * Y_HALF)
+        scalar_copy, vector_copy = nc.scalar.copy, nc.vector.tensor_copy
+        copy_for = {
+            "words_x": lambda i: vector_copy,
+            "words_c": lambda i: vector_copy if i < 6 else scalar_copy,
+            "group_x": lambda i: scalar_copy,
+            "group_c": lambda i: (scalar_copy, vector_copy)[i % 2],
+            "group_r": lambda i: (scalar_copy, vector_copy)[i % 2],
+            "copy_out": lambda n: (vector_copy, scalar_copy, scalar_copy, scalar_copy)[n],
+        }
+
+        def words_x(i, n):
+            x_words[i] = order_words(copy_for["words_x"](i), x_raw[i], G, "x_words")
+
+        def words_c(i, n):
+            c_words[i] = order_words(copy_for["words_c"](i), c_raw[i], 1, "c_words")
+
+        def turn_x(i, n):
+            x_ps[i] = transpose_words(x_words[i], 4)
+
+        def turn_c(i, n):
+            c_ps[i] = transpose_words(c_words[i], 2)
+
+        def group_x(i, n):
+            x_grp[i] = interleave(copy_for["group_x"](i), x_ps[i], G, "x_grp")
+
+        def group_c(i, n):
+            c_grp[i] = interleave(copy_for["group_c"](i), c_ps[i], 1, "c_grp")
+
+        def quantise_x(i, n):
+            x_q[i] = quantise(x_grp[i], G, "x")
+
+        def quantise_c(i, n):
+            c_q[i] = quantise(c_grp[i], 1, "c")
+
+        def y_group(h):
+            if h not in y_grp:
+                t = keep.tile([P, NB, 4], BF16, tag="y_grp", name="y_grp", bufs=2, align_bytes=64)
+                y_grp[h] = t
+            return y_grp[h]
+
+        def y_vector(h, n):
+            lo = h * NB
+            nc.vector.tensor_copy(out=y_group(h)[:, :Y_V, :], in_=y_raw[:, :, lo:lo + Y_V].rearrange("p t n -> p n t"))
+
+        def y_scalar(h, n):
+            lo, hi = h * NB + Y_V, (h + 1) * NB
+            nc.scalar.copy(out=y_group(h)[:, Y_V:, :], in_=y_raw[:, :, lo:hi].rearrange("p t n -> p n t"))
+
+        def quantise_y(h, n):
+            cols = slice(h * NB, (h + 1) * NB)
             nc.vector.quantize_mx(
-                out=y_codes[:, cols].bitcast(FP8X4), scales=y_sc[:, cols], in_=y_grp[h][:].rearrange("p n j -> p (n j)"))
+                out=y_codes[:, cols].bitcast(FP8X4), scales=y_sc[:, cols], in_=y_grp[h][:].rearrange("p n t -> p (n t)"))
 
-        def mm_xa(i):
-            codes, scales = x_q[i]
-            for n in range(2):
-                t = psum.tile([P, NB], F32, tag="acc", name="acc", bufs=5)
-                for g in range(G):
-                    nc.tensor.matmul_mx(
-                        out=t[:],
-                        lhsT=codes[:, g * P:(g + 1) * P].bitcast(FP8X4),
-                        lhsT_scale=scales[:, g * P:(g + 1) * P],
-                        rhs=a_sb[:, g, 2 * NB * n:2 * NB * (n + 1)].bitcast(FP4X4),
-                        rhs_scale=a_sc[:, g, NB * n:NB * (n + 1)],
-                        start=(g == 0),
-                        stop=False,
-                    )
-                l_ps[i, n] = t
+        def across(i, n):
+            l_ps[i, n] = new_bank()
+            for g in range(G):
+                mx_pass(l_ps[i, n], x_q[i], g, a_sb[:, g, 2 * NB * n:2 * NB * (n + 1)], FP4X4,
+                        a_sc[:, g, NB * n:NB * (n + 1)], start=(g == 0), stop=False)
 
-        def mm_cy(i):
-            codes, scales = c_q[i]
-            for n in range(2):
-                nc.tensor.matmul_mx(
-                    out=l_ps[i, n][:],
-                    lhsT=codes[:].bitcast(FP8X4),
-                    lhsT_scale=scales[:],
-                    rhs=y_codes[:, NB * n:NB * (n + 1)].bitcast(FP8X4),
-                    rhs_scale=y_sc[:, NB * n:NB * (n + 1)],
-                    start=False,
-                    stop=True,
-                )
+        def along(i, n):
+            cols = slice(NB * n, NB * (n + 1))
+            mx_pass(l_ps[i, n], c_q[i], 0, y_codes[:, cols], FP8X4, y_sc[:, cols], start=False, stop=True)
 
-        def mm_layer1(i):
-            codes, scales = x_q[i]
-            c_codes, c_scales = c_q[i]
-            for n in range(2):
-                t = psum.tile([P, NB], F32, tag="acc", name="acc", bufs=5)
-                for g in range(G):
-                    nc.tensor.matmul_mx(
-                        out=t[:],
-                        lhsT=codes[:, g * P:(g + 1) * P].bitcast(FP8X4),
-                        lhsT_scale=scales[:, g * P:(g + 1) * P],
-                        rhs=a_sb[:, g, 2 * NB * n:2 * NB * (n + 1)].bitcast(FP4X4),
-                        rhs_scale=a_sc[:, g, NB * n:NB * (n + 1)],
-                        start=(g == 0),
-                        stop=False,
-                    )
-                nc.tensor.matmul_mx(
-                    out=t[:],
-                    lhsT=c_codes[:].bitcast(FP8X4),
-                    lhsT_scale=c_scales[:],
-                    rhs=y_codes[:, NB * n:NB * (n + 1)].bitcast(FP8X4),
-                    rhs_scale=y_sc[:, NB * n:NB * (n + 1)],
-                    start=False,
-                    stop=True,
-                )
-                l_ps[i, n] = t
-
-        def inverse_background(i, n):
-            t = work.tile([P, NB], F32, tag="inv_bg", name="inv_bg", bufs=6)
+        def inverse(i, n):
+            t = work.tile([P, NB], F32, tag="inv_bg", name="inv_bg", bufs=8)
             nc.scalar.activation(out=t[:], in_=l_ps[i, n][:], func=EXP, scale=-1.0)
             inv_bg[i, n] = t
 
-        def multiply(i, n):
-            if n == 0:
-                r = work.tile([P, B], BF16, tag="r_words", name="r_words")
-                r_words[i] = r
+        def ratio(i, n):
+            if i not in r_words:
+                t = work.tile([P, B], BF16, tag="r_words", name="r_words", bufs=6)
+                r_words[i] = t
             cols = slice(n * NB, (n + 1) * NB)
             nc.vector.tensor_tensor(
                 out=r_words[i][:, cols].rearrange("p (u m h) -> p u m h", u=2, h=2),
@@ -196,279 +195,324 @@ def tile_bearing_time_normaliser_s3_kernel(tc, x, a_words, a_scales, c, y, e, w_
                 op=MULT,
             )
 
-        def mm_layer2(i, n):
-            codes, scales = r_q[i]
-            t = psum.tile([P, NB], F32, tag="acc", name="acc", bufs=5)
+        def turn_r(i, n):
+            r_ps[i] = transpose_words(r_words[i][:].bitcast(F32), 4)
+
+        def group_r(i, n):
+            r_grp[i] = interleave(copy_for["group_r"](i), r_ps[i], G, "r_grp")
+
+        def quantise_r(i, n):
+            r_q[i] = quantise(r_grp[i], G, "r")
+
+        def detect(i, n):
+            o_ps[i, n] = new_bank()
             for g in range(G):
-                nc.tensor.matmul_mx(
-                    out=t[:],
-                    lhsT=codes[:, g * P:(g + 1) * P].bitcast(FP8X4),
-                    lhsT_scale=scales[:, g * P:(g + 1) * P],
-                    rhs=w_sb[n // 2][:, g, 2 * NB * (n % 2):2 * NB * (n % 2 + 1)].bitcast(FP4X4),
-                    rhs_scale=w_sc[:, g, NB * n:NB * (n + 1)],
-                    start=(g == 0),
-                    stop=(g == G - 1),
-                )
-            o_ps[i, n] = t
+                mx_pass(o_ps[i, n], r_q[i], g, w_sb[n // 2][:, g, 2 * NB * (n % 2):2 * NB * (n % 2 + 1)], FP4X4,
+                        w_sc[:, g, NB * n:NB * (n + 1)], start=(g == 0), stop=(g == G - 1))
 
         def store(i, lo, hi):
-            nc.sync.dma_start(out=out[i * P:(i + 1) * P, lo:hi], in_=o_sb[i][:, lo:hi])
+            nc.sync.dma_start(out=out_rows[:, i, lo:hi], in_=o_sb[i][:, lo:hi])
 
         def copy_out(i, n):
-            if n == 0:
-                o = work.tile([P, D], F32, tag="o_sb", name="o_sb")
-                o_sb[i] = o
-            lo, mid, hi = n * NB, n * NB + NB // 2, (n + 1) * NB
+            if i not in o_sb:
+                t = work.tile([P, D], F32, tag="o_sb", name="o_sb", bufs=4)
+                o_sb[i] = t
             if (i, n) == (TILES - 1, 3):
-                nc.scalar.copy(out=o_sb[i][:, lo:mid], in_=o_ps[i, n][:, :NB // 2])
-                store(i, lo, mid)
-                nc.vector.tensor_copy(out=o_sb[i][:, mid:hi], in_=o_ps[i, n][:, NB // 2:])
-                store(i, mid, hi)
                 return
-            copy = nc.scalar.copy if n % 2 == 0 else nc.vector.tensor_copy
-            copy(out=o_sb[i][:, lo:hi], in_=o_ps[i, n][:])
-            if i == TILES - 1:
-                store(i, lo, hi)
-            elif n % 2 == 1:
-                store(i, lo - NB, hi)
+            copy_for["copy_out"](n)(out=o_sb[i][:, n * NB:(n + 1) * NB], in_=o_ps[i, n][:])
 
-        nc.vector.memset(a_sc[:].rearrange("p g n -> p (g n)").bitcast(I32), 0)
+        def store_pair(i, n):
+            store(i, (n - 1) * NB, (n + 1) * NB)
+
+        def store_one(i, n):
+            store(i, n * NB, (n + 1) * NB)
+
+        def last_bank(h, n):
+            lo = 3 * NB + h * (NB // 2)
+            copy = (scalar_copy, vector_copy)[h]
+            copy(out=o_sb[TILES - 1][:, lo:lo + NB // 2], in_=o_ps[TILES - 1, 3][:, h * (NB // 2):(h + 1) * (NB // 2)])
+
+        def last_store(h, n):
+            lo = 3 * NB + h * (NB // 2)
+            store(TILES - 1, lo, lo + NB // 2)
+
+        def warm_up(j, n):
+            bank = new_bank()
+            nc.tensor.matmul_mx(
+                out=bank[:], lhsT=y_codes[:, :P].bitcast(FP8X4), lhsT_scale=y_sc[:, :P],
+                rhs=y_codes[:, :NB].bitcast(FP8X4), rhs_scale=y_sc[:, :NB], start=True, stop=True)
+
+        nc.vector.memset(y_codes[:, :NB].bitcast(I32), 0)
+        nc.vector.memset(y_sc[:, :NB].bitcast(I32), 0)
         nc.vector.memset(warm_in[:], 0.0)
+        nc.vector.memset(a_sc[:].rearrange("p g n -> p (g n)").bitcast(I32), 0)
         nc.vector.memset(w_sc[:].rearrange("p g n -> p (g n)").bitcast(I32), 0)
         make_identity(nc, ident[:])
         nc.scalar.activation(out=warm_out[:], in_=warm_in[:], func=EXP, scale=-1.0)
 
-        def load_w(h):
-            nc.sync.dma_start(
-                out=w_sb[h][:].bitcast(I32),
-                in_=w_words[:, :, h * D:(h + 1) * D].rearrange("g p n -> p g n").bitcast(I32))
-
-        def transpose_x(i, tag="xt"):
-            x_ps[i] = transpose_words(x_words[i], 4, tag)
-
-        def transpose_c(i, tag="ct"):
-            c_ps[i] = transpose_words(c_words[i], 2, tag)
-
-        def gather_x(i, copy=nc.scalar.copy):
-            x_grp[i] = gather_words(copy, x_ps[i], 2, "x_grp")
-
-        def gather_c(i, copy=nc.scalar.copy):
-            c_grp[i] = gather_words(copy, c_ps[i], 1, "c_grp")
-
-        def quantise_x(i):
-            x_q[i] = quantise(x_grp[i], 2, "x")
-
-        def quantise_c(i):
-            c_q[i] = quantise(c_grp[i], 1, "c")
-
-        def transpose_r(i):
-            tag = "xt" if i == TILES - 2 else "rt"
-            r_ps[i] = transpose_words(r_words[i][:].bitcast(F32), 4, tag)
-
-        def gather_r(i):
-            r_grp[i] = gather_words(nc.vector.tensor_copy, r_ps[i], 2, "r_grp")
-
-        def quantise_r(i):
-            r_q[i] = quantise(r_grp[i], 2, "r")
-
-        def layer2(i, n):
-            mm_layer2(i, n)
-            copy_out(i, n)
-
-        vcopy = nc.vector.tensor_copy
-        load_c(0)
-        load_x(0)
-        load_y(0)
-        load_scales(nc.sync, a_sc, a_scales)
-        load_y(1)
+        load_rows(x, x_raw, "x_raw", 0, 2)
+        load_rows(x, x_raw, "x_raw", 2, 4)
+        load_scales(a_sc, a_scales)
+        load_rows(x, x_raw, "x_raw", 4, 6)
+        load_rows(c, c_raw, "c_raw", 0, 4)
         nc.sync.dma_start(out=a_sb[:].bitcast(I32), in_=a_words.rearrange("g p n -> p g n").bitcast(I32))
-        load_x(1)
-        load_c(1)
-        load_x(3)
-        load_x(2)
-        load_c(4)
-        load_c(2)
-        load_x(4)
-        load_e(2)
-        load_c(3)
-        load_scales(nc.gpsimd, w_sc, w_scales)
-        load_e(0)
-        load_e(1)
-        load_w(0)
+        nc.sync.dma_start(out=y_raw[:], in_=y.rearrange("(p t) n -> p t n", t=4))
+        load_rows(c, c_raw, "c_raw", 4, 8)
+        load_rows(e, e_raw, "e_raw", 2, 4)
+        load_rows(x, x_raw, "x_raw", 6, 8)
+        load_rows(e, e_raw, "e_raw", 0, 2)
+        load_rows(e, e_raw, "e_raw", 4, 6)
+        load_scales(w_sc, w_scales)
         load_w(1)
-        load_e(3)
-        load_x(5)
-        load_c(5)
-        load_e(4)
-        load_x(6)
-        load_c(6)
-        load_e(5)
-        load_x(7)
-        load_c(7)
-        load_e(6)
-        load_e(7)
-        permute_c(0, vcopy)
-        permute_x(0, vcopy)
-        transpose_x(0)
-        gather_x(0)
-        y_interleave(0)
-        transpose_c(0)
-        quantise_x(0)
-        y_interleave(1)
-        mm_xa(0)
-        permute_x(1, vcopy)
-        y_quantise(0)
-        permute_c(1, vcopy)
-        transpose_x(1)
-        gather_c(0)
-        quantise_c(0)
-        y_quantise(1)
-        permute_x(2, vcopy)
-        transpose_c(1)
-        mm_cy(0)
-        transpose_x(2)
-        permute_c(2, vcopy)
-        gather_x(1)
-        gather_c(1)
-        transpose_c(2)
-        quantise_x(1)
-        permute_x(3, vcopy)
-        inverse_background(0, 0)
-        quantise_c(1)
-        gather_c(2)
-        permute_c(3, vcopy)
-        multiply(0, 0)
-        mm_layer1(1)
-        transpose_c(3)
-        quantise_c(2)
-        inverse_background(0, 1)
-        gather_x(2)
-        inverse_background(1, 0)
-        transpose_x(3)
-        gather_x(3)
-        multiply(0, 1)
-        gather_c(3)
-        quantise_x(2)
-        inverse_background(1, 1)
-        transpose_r(0)
-        multiply(1, 0)
-        mm_layer1(2)
-        gather_r(0)
-        inverse_background(2, 0)
-        inverse_background(2, 1)
-        quantise_x(3)
-        quantise_r(0)
-        layer2(0, 0)
-        multiply(1, 1)
-        quantise_c(3)
-        multiply(2, 0)
-        multiply(2, 1)
-        permute_c(4)
-        permute_x(4)
-        layer2(0, 1)
-        layer2(0, 2)
-        layer2(0, 3)
-        transpose_r(1)
-        transpose_x(4)
-        transpose_c(4)
-        gather_r(1)
-        gather_x(4)
-        gather_c(4)
-        quantise_r(1)
-        quantise_x(4)
-        quantise_c(4)
-        mm_layer1(3)
-        inverse_background(3, 0)
-        permute_c(5)
-        inverse_background(3, 1)
-        multiply(3, 0)
-        multiply(3, 1)
-        layer2(1, 0)
-        permute_x(5)
-        layer2(1, 1)
-        layer2(1, 2)
-        layer2(1, 3)
-        transpose_r(2)
-        transpose_x(5)
-        transpose_c(5)
-        gather_r(2)
-        gather_x(5)
-        gather_c(5)
-        quantise_r(2)
-        quantise_x(5)
-        quantise_c(5)
-        mm_layer1(4)
-        inverse_background(4, 0)
-        permute_c(6)
-        inverse_background(4, 1)
-        multiply(4, 0)
-        multiply(4, 1)
-        layer2(2, 0)
-        permute_x(6)
-        layer2(2, 1)
-        layer2(2, 2)
-        layer2(2, 3)
-        transpose_r(3)
-        transpose_x(6)
-        transpose_c(6)
-        gather_r(3)
-        gather_x(6)
-        gather_c(6)
-        quantise_r(3)
-        quantise_x(6)
-        quantise_c(6)
-        mm_layer1(5)
-        inverse_background(5, 0)
-        permute_c(7)
-        inverse_background(5, 1)
-        multiply(5, 0)
-        multiply(5, 1)
-        layer2(3, 0)
-        permute_x(7)
-        layer2(3, 1)
-        layer2(3, 2)
-        layer2(3, 3)
-        transpose_r(4)
-        transpose_x(7)
-        transpose_c(7)
-        gather_r(4)
-        gather_x(7)
-        gather_c(7)
-        quantise_r(4)
-        quantise_x(7)
-        quantise_c(7)
-        mm_layer1(6)
-        inverse_background(6, 0)
-        inverse_background(6, 1)
-        multiply(6, 0)
-        multiply(6, 1)
-        layer2(4, 0)
-        layer2(4, 1)
-        layer2(4, 2)
-        layer2(4, 3)
-        transpose_r(5)
-        transpose_r(6)
-        gather_r(5)
-        gather_r(6)
-        quantise_r(5)
-        quantise_r(6)
-        mm_layer1(7)
-        inverse_background(7, 0)
-        inverse_background(7, 1)
-        multiply(7, 0)
-        multiply(7, 1)
-        layer2(5, 0)
-        layer2(5, 1)
-        layer2(5, 2)
-        layer2(5, 3)
-        transpose_r(7)
-        gather_r(7)
-        quantise_r(7)
-        layer2(6, 0)
-        layer2(6, 1)
-        layer2(6, 2)
-        layer2(6, 3)
-        layer2(7, 0)
-        layer2(7, 1)
-        layer2(7, 2)
-        layer2(7, 3)
+        load_w(0)
+        load_rows(e, e_raw, "e_raw", 6, 8)
+        warm_up(1, 0)
+        warm_up(2, 0)
+        warm_up(4, 0)
+        warm_up(7, 0)
+        words_x(0, 0)
+        words_x(1, 0)
+        warm_up(0, 0)
+        words_x(2, 0)
+        words_x(3, 0)
+        turn_x(0, 0)
+        turn_x(1, 0)
+        turn_x(2, 0)
+        turn_x(3, 0)
+        warm_up(3, 0)
+        group_x(0, 0)
+        group_x(1, 0)
+        words_x(4, 0)
+        words_x(5, 0)
+        warm_up(5, 0)
+        words_c(2, 0)
+        words_c(3, 0)
+        words_c(0, 0)
+        words_c(1, 0)
+        warm_up(6, 0)
+        quantise_x(0, 0)
+        quantise_x(1, 0)
+        turn_x(4, 0)
+        turn_x(5, 0)
+        group_x(2, 0)
+        group_x(3, 0)
+        turn_c(2, 0)
+        turn_c(3, 0)
+        quantise_x(2, 0)
+        quantise_x(3, 0)
+        group_c(2, 0)
+        group_c(3, 0)
+        turn_c(0, 0)
+        turn_c(1, 0)
+        group_c(0, 0)
+        group_c(1, 0)
+        group_x(4, 0)
+        group_x(5, 0)
+        across(0, 1)
+        across(1, 1)
+        quantise_c(2, 0)
+        quantise_c(3, 0)
+        quantise_c(0, 0)
+        quantise_c(1, 0)
+        y_scalar(1, 0)
+        y_vector(1, 0)
+        y_scalar(0, 0)
+        quantise_y(1, 0)
+        y_vector(0, 0)
+        across(2, 1)
+        across(3, 1)
+        across(0, 0)
+        across(1, 0)
+        along(0, 1)
+        along(1, 1)
+        words_c(4, 0)
+        words_c(5, 0)
+        quantise_y(0, 0)
+        quantise_x(4, 0)
+        quantise_x(5, 0)
+        along(2, 1)
+        along(3, 1)
+        words_c(6, 0)
+        words_c(7, 0)
+        words_x(6, 0)
+        words_x(7, 0)
+        inverse(0, 1)
+        inverse(1, 1)
+        across(2, 0)
+        across(3, 0)
+        inverse(2, 1)
+        inverse(3, 1)
+        along(0, 0)
+        along(1, 0)
+        along(2, 0)
+        along(3, 0)
+        ratio(2, 1)
+        ratio(3, 1)
+        ratio(0, 1)
+        ratio(1, 1)
+        turn_c(4, 0)
+        turn_c(5, 0)
+        inverse(0, 0)
+        inverse(1, 0)
+        turn_c(6, 0)
+        turn_c(7, 0)
+        inverse(2, 0)
+        inverse(3, 0)
+        group_c(4, 0)
+        group_c(5, 0)
+        turn_x(6, 0)
+        turn_x(7, 0)
+        group_c(6, 0)
+        group_c(7, 0)
+        quantise_c(4, 0)
+        quantise_c(5, 0)
+        across(4, 0)
+        across(5, 0)
+        ratio(0, 0)
+        ratio(1, 0)
+        across(4, 1)
+        across(5, 1)
+        group_x(6, 0)
+        group_x(7, 0)
+        along(4, 1)
+        along(5, 1)
+        along(4, 0)
+        along(5, 0)
+        turn_r(0, 0)
+        turn_r(1, 0)
+        inverse(4, 0)
+        inverse(5, 0)
+        ratio(2, 0)
+        ratio(3, 0)
+        quantise_x(6, 0)
+        quantise_x(7, 0)
+        inverse(4, 1)
+        inverse(5, 1)
+        quantise_c(6, 0)
+        quantise_c(7, 0)
+        turn_r(2, 0)
+        turn_r(3, 0)
+        group_r(2, 0)
+        group_r(3, 0)
+        group_r(0, 0)
+        group_r(1, 0)
+        ratio(4, 0)
+        ratio(5, 0)
+        across(6, 1)
+        across(7, 1)
+        along(6, 1)
+        along(7, 1)
+        quantise_r(2, 0)
+        quantise_r(3, 0)
+        across(6, 0)
+        across(7, 0)
+        along(6, 0)
+        along(7, 0)
+        inverse(6, 0)
+        inverse(7, 0)
+        inverse(6, 1)
+        inverse(7, 1)
+        quantise_r(0, 0)
+        quantise_r(1, 0)
+        detect(2, 0)
+        detect(2, 1)
+        ratio(6, 0)
+        ratio(7, 0)
+        detect(0, 0)
+        detect(0, 1)
+        copy_out(2, 0)
+        copy_out(2, 1)
+        detect(2, 2)
+        detect(2, 3)
+        copy_out(2, 2)
+        copy_out(2, 3)
+        copy_out(0, 0)
+        copy_out(0, 1)
+        detect(3, 2)
+        detect(3, 3)
+        ratio(4, 1)
+        ratio(5, 1)
+        ratio(6, 1)
+        ratio(7, 1)
+        detect(0, 2)
+        detect(0, 3)
+        detect(3, 0)
+        detect(3, 1)
+        store_pair(2, 1)
+        copy_out(0, 2)
+        copy_out(0, 3)
+        copy_out(3, 2)
+        copy_out(3, 3)
+        detect(1, 0)
+        detect(1, 1)
+        copy_out(3, 0)
+        copy_out(3, 1)
+        copy_out(1, 0)
+        copy_out(1, 1)
+        store_pair(2, 3)
+        store_pair(0, 1)
+        turn_r(4, 0)
+        turn_r(5, 0)
+        turn_r(6, 0)
+        turn_r(7, 0)
+        group_r(4, 0)
+        group_r(5, 0)
+        store_pair(0, 3)
+        quantise_r(4, 0)
+        quantise_r(5, 0)
+        group_r(6, 0)
+        group_r(7, 0)
+        store_pair(3, 3)
+        detect(1, 2)
+        detect(1, 3)
+        copy_out(1, 2)
+        copy_out(1, 3)
+        detect(4, 0)
+        detect(4, 1)
+        copy_out(4, 0)
+        copy_out(4, 1)
+        store_pair(3, 1)
+        quantise_r(6, 0)
+        quantise_r(7, 0)
+        detect(5, 2)
+        detect(5, 3)
+        detect(5, 0)
+        detect(5, 1)
+        store_pair(1, 1)
+        detect(7, 0)
+        detect(7, 1)
+        copy_out(5, 2)
+        copy_out(5, 3)
+        detect(4, 2)
+        detect(4, 3)
+        copy_out(5, 0)
+        copy_out(5, 1)
+        copy_out(7, 0)
+        copy_out(7, 1)
+        detect(6, 0)
+        detect(6, 1)
+        store_pair(1, 3)
+        copy_out(4, 2)
+        copy_out(4, 3)
+        copy_out(6, 0)
+        copy_out(6, 1)
+        detect(6, 2)
+        detect(6, 3)
+        detect(7, 2)
+        detect(7, 3)
+        store_pair(4, 1)
+        store_pair(5, 3)
+        store_pair(5, 1)
+        copy_out(6, 2)
+        copy_out(6, 3)
+        store_one(7, 0)
+        last_bank(0, 0)
+        store_one(7, 1)
+        store_pair(4, 3)
+        last_bank(1, 0)
+        store_pair(6, 1)
+        store_pair(6, 3)
+        last_store(1, 0)
+        last_store(0, 0)
+        copy_out(7, 2)
+        store_one(7, 2)

@@ -118,11 +118,11 @@ def tile_bearing_time_normaliser_s3_kernel(tc, x, a_words, a_scales, c, y, e, w_
         scalar_copy, vector_copy = nc.scalar.copy, nc.vector.tensor_copy
         copy_for = {
             "words_x": lambda i: vector_copy,
-            "words_c": lambda i: vector_copy if i < 6 else scalar_copy,
+            "words_c": lambda i: vector_copy if i < 2 else scalar_copy,
             "group_x": lambda i: scalar_copy,
-            "group_c": lambda i: (scalar_copy, vector_copy)[i % 2],
-            "group_r": lambda i: (scalar_copy, vector_copy)[i % 2],
-            "copy_out": lambda n: (vector_copy, scalar_copy, scalar_copy, scalar_copy)[n],
+            "group_c": lambda i: scalar_copy,
+            "group_r": lambda i: (vector_copy, scalar_copy)[i % 2],
+            "copy_out": lambda n: (vector_copy, scalar_copy, scalar_copy, vector_copy)[n],
         }
 
         def words_x(i, n):
@@ -250,269 +250,271 @@ def tile_bearing_time_normaliser_s3_kernel(tc, x, a_words, a_scales, c, y, e, w_
         make_identity(nc, ident[:])
         nc.scalar.activation(out=warm_out[:], in_=warm_in[:], func=EXP, scale=-1.0)
 
-        load_rows(x, x_raw, "x_raw", 0, 2)
-        load_rows(x, x_raw, "x_raw", 2, 4)
-        load_scales(a_sc, a_scales)
-        load_rows(x, x_raw, "x_raw", 4, 6)
         load_rows(c, c_raw, "c_raw", 0, 4)
+        load_rows(c, c_raw, "c_raw", 4, 8)
+        load_rows(x, x_raw, "x_raw", 2, 4)
+        load_rows(x, x_raw, "x_raw", 4, 6)
+        load_scales(a_sc, a_scales)
         nc.sync.dma_start(out=a_sb[:].bitcast(I32), in_=a_words.rearrange("g p n -> p g n").bitcast(I32))
         nc.sync.dma_start(out=y_raw[:], in_=y.rearrange("(p t) n -> p t n", t=4))
-        load_rows(c, c_raw, "c_raw", 4, 8)
-        load_rows(e, e_raw, "e_raw", 2, 4)
-        load_rows(x, x_raw, "x_raw", 6, 8)
+        load_rows(x, x_raw, "x_raw", 0, 2)
         load_rows(e, e_raw, "e_raw", 0, 2)
         load_rows(e, e_raw, "e_raw", 4, 6)
-        load_scales(w_sc, w_scales)
-        load_w(1)
-        load_w(0)
+        load_rows(x, x_raw, "x_raw", 6, 8)
         load_rows(e, e_raw, "e_raw", 6, 8)
-        warm_up(1, 0)
-        warm_up(2, 0)
+        load_rows(e, e_raw, "e_raw", 2, 4)
+        load_w(1)
+        load_scales(w_sc, w_scales)
+        load_w(0)
         warm_up(4, 0)
-        warm_up(7, 0)
-        words_x(0, 0)
-        words_x(1, 0)
-        warm_up(0, 0)
-        words_x(2, 0)
-        words_x(3, 0)
-        turn_x(0, 0)
-        turn_x(1, 0)
-        turn_x(2, 0)
-        turn_x(3, 0)
-        warm_up(3, 0)
-        group_x(0, 0)
-        group_x(1, 0)
-        words_x(4, 0)
-        words_x(5, 0)
-        warm_up(5, 0)
         words_c(2, 0)
         words_c(3, 0)
-        words_c(0, 0)
-        words_c(1, 0)
-        warm_up(6, 0)
-        quantise_x(0, 0)
-        quantise_x(1, 0)
-        turn_x(4, 0)
-        turn_x(5, 0)
-        group_x(2, 0)
-        group_x(3, 0)
-        turn_c(2, 0)
-        turn_c(3, 0)
-        quantise_x(2, 0)
-        quantise_x(3, 0)
-        group_c(2, 0)
-        group_c(3, 0)
-        turn_c(0, 0)
-        turn_c(1, 0)
-        group_c(0, 0)
-        group_c(1, 0)
-        group_x(4, 0)
-        group_x(5, 0)
-        across(0, 1)
-        across(1, 1)
-        quantise_c(2, 0)
-        quantise_c(3, 0)
-        quantise_c(0, 0)
-        quantise_c(1, 0)
-        y_scalar(1, 0)
-        y_vector(1, 0)
-        y_scalar(0, 0)
-        quantise_y(1, 0)
-        y_vector(0, 0)
-        across(2, 1)
-        across(3, 1)
-        across(0, 0)
-        across(1, 0)
-        along(0, 1)
-        along(1, 1)
-        words_c(4, 0)
-        words_c(5, 0)
-        quantise_y(0, 0)
-        quantise_x(4, 0)
-        quantise_x(5, 0)
-        along(2, 1)
-        along(3, 1)
         words_c(6, 0)
         words_c(7, 0)
-        words_x(6, 0)
-        words_x(7, 0)
-        inverse(0, 1)
-        inverse(1, 1)
-        across(2, 0)
-        across(3, 0)
-        inverse(2, 1)
-        inverse(3, 1)
-        along(0, 0)
-        along(1, 0)
-        along(2, 0)
-        along(3, 0)
-        ratio(2, 1)
-        ratio(3, 1)
-        ratio(0, 1)
-        ratio(1, 1)
-        turn_c(4, 0)
-        turn_c(5, 0)
-        inverse(0, 0)
-        inverse(1, 0)
+        warm_up(1, 0)
+        warm_up(7, 0)
+        warm_up(5, 0)
+        turn_c(2, 0)
+        turn_c(3, 0)
+        warm_up(3, 0)
+        warm_up(6, 0)
+        group_c(2, 0)
+        group_c(3, 0)
         turn_c(6, 0)
         turn_c(7, 0)
-        inverse(2, 0)
-        inverse(3, 0)
-        group_c(4, 0)
-        group_c(5, 0)
-        turn_x(6, 0)
-        turn_x(7, 0)
+        words_c(0, 0)
+        words_c(1, 0)
+        words_x(2, 0)
+        words_x(3, 0)
+        words_x(4, 0)
+        words_x(5, 0)
+        warm_up(0, 0)
+        warm_up(2, 0)
+        turn_x(2, 0)
+        turn_x(3, 0)
+        quantise_c(2, 0)
+        quantise_c(3, 0)
+        words_c(4, 0)
+        words_c(5, 0)
         group_c(6, 0)
         group_c(7, 0)
-        quantise_c(4, 0)
-        quantise_c(5, 0)
-        across(4, 0)
-        across(5, 0)
-        ratio(0, 0)
-        ratio(1, 0)
-        across(4, 1)
-        across(5, 1)
-        group_x(6, 0)
-        group_x(7, 0)
-        along(4, 1)
-        along(5, 1)
-        along(4, 0)
-        along(5, 0)
-        turn_r(0, 0)
-        turn_r(1, 0)
-        inverse(4, 0)
-        inverse(5, 0)
-        ratio(2, 0)
-        ratio(3, 0)
-        quantise_x(6, 0)
-        quantise_x(7, 0)
-        inverse(4, 1)
-        inverse(5, 1)
+        turn_x(4, 0)
+        turn_x(5, 0)
+        turn_c(4, 0)
+        turn_c(5, 0)
+        group_x(2, 0)
+        group_x(3, 0)
+        group_x(4, 0)
+        group_x(5, 0)
+        group_c(4, 0)
+        group_c(5, 0)
         quantise_c(6, 0)
         quantise_c(7, 0)
-        turn_r(2, 0)
-        turn_r(3, 0)
-        group_r(2, 0)
-        group_r(3, 0)
-        group_r(0, 0)
-        group_r(1, 0)
+        y_scalar(0, 0)
+        turn_c(0, 0)
+        turn_c(1, 0)
+        quantise_x(2, 0)
+        quantise_x(3, 0)
+        quantise_x(4, 0)
+        quantise_x(5, 0)
+        y_scalar(1, 0)
+        y_vector(0, 0)
+        group_c(0, 0)
+        group_c(1, 0)
+        quantise_y(0, 0)
+        across(2, 0)
+        across(3, 0)
+        across(4, 0)
+        across(5, 0)
+        words_x(0, 0)
+        words_x(1, 0)
+        across(2, 1)
+        across(3, 1)
+        y_vector(1, 0)
+        along(2, 0)
+        along(3, 0)
+        inverse(2, 0)
+        inverse(3, 0)
+        quantise_c(4, 0)
+        quantise_c(5, 0)
+        turn_x(0, 0)
+        turn_x(1, 0)
+        group_x(0, 0)
+        group_x(1, 0)
+        across(4, 1)
+        across(5, 1)
+        quantise_y(1, 0)
+        along(4, 0)
+        along(5, 0)
+        along(4, 1)
+        along(5, 1)
+        along(2, 1)
+        along(3, 1)
+        inverse(4, 0)
+        inverse(5, 0)
+        inverse(2, 1)
+        inverse(3, 1)
+        quantise_c(0, 0)
+        quantise_c(1, 0)
+        quantise_x(0, 0)
+        quantise_x(1, 0)
+        across(0, 0)
+        across(1, 0)
+        along(0, 0)
+        along(1, 0)
+        words_x(6, 0)
+        words_x(7, 0)
         ratio(4, 0)
         ratio(5, 0)
-        across(6, 1)
-        across(7, 1)
-        along(6, 1)
-        along(7, 1)
-        quantise_r(2, 0)
-        quantise_r(3, 0)
-        across(6, 0)
-        across(7, 0)
-        along(6, 0)
-        along(7, 0)
-        inverse(6, 0)
-        inverse(7, 0)
-        inverse(6, 1)
-        inverse(7, 1)
-        quantise_r(0, 0)
-        quantise_r(1, 0)
-        detect(2, 0)
-        detect(2, 1)
-        ratio(6, 0)
-        ratio(7, 0)
-        detect(0, 0)
-        detect(0, 1)
-        copy_out(2, 0)
-        copy_out(2, 1)
-        detect(2, 2)
-        detect(2, 3)
-        copy_out(2, 2)
-        copy_out(2, 3)
-        copy_out(0, 0)
-        copy_out(0, 1)
-        detect(3, 2)
-        detect(3, 3)
+        ratio(2, 0)
+        ratio(3, 0)
+        turn_x(6, 0)
+        turn_x(7, 0)
+        inverse(4, 1)
+        inverse(5, 1)
+        across(0, 1)
+        across(1, 1)
+        along(0, 1)
+        along(1, 1)
+        ratio(2, 1)
+        ratio(3, 1)
         ratio(4, 1)
         ratio(5, 1)
-        ratio(6, 1)
-        ratio(7, 1)
-        detect(0, 2)
-        detect(0, 3)
-        detect(3, 0)
-        detect(3, 1)
-        store_pair(2, 1)
-        copy_out(0, 2)
-        copy_out(0, 3)
-        copy_out(3, 2)
-        copy_out(3, 3)
-        detect(1, 0)
-        detect(1, 1)
-        copy_out(3, 0)
-        copy_out(3, 1)
-        copy_out(1, 0)
-        copy_out(1, 1)
-        store_pair(2, 3)
-        store_pair(0, 1)
+        group_x(6, 0)
+        group_x(7, 0)
+        turn_r(2, 0)
+        turn_r(3, 0)
+        inverse(0, 0)
+        inverse(1, 0)
+        inverse(0, 1)
+        inverse(1, 1)
         turn_r(4, 0)
         turn_r(5, 0)
-        turn_r(6, 0)
-        turn_r(7, 0)
+        quantise_x(6, 0)
+        quantise_x(7, 0)
         group_r(4, 0)
         group_r(5, 0)
-        store_pair(0, 3)
+        group_r(2, 0)
+        group_r(3, 0)
+        across(6, 0)
+        across(7, 0)
         quantise_r(4, 0)
         quantise_r(5, 0)
-        group_r(6, 0)
-        group_r(7, 0)
-        store_pair(3, 3)
-        detect(1, 2)
-        detect(1, 3)
-        copy_out(1, 2)
-        copy_out(1, 3)
-        detect(4, 0)
-        detect(4, 1)
-        copy_out(4, 0)
-        copy_out(4, 1)
-        store_pair(3, 1)
-        quantise_r(6, 0)
-        quantise_r(7, 0)
+        along(6, 0)
+        along(7, 0)
+        across(6, 1)
+        across(7, 1)
+        quantise_r(2, 0)
+        quantise_r(3, 0)
+        along(6, 1)
+        along(7, 1)
         detect(5, 2)
         detect(5, 3)
+        ratio(0, 1)
+        ratio(1, 1)
+        inverse(6, 1)
+        inverse(7, 1)
+        inverse(6, 0)
+        inverse(7, 0)
+        ratio(0, 0)
+        ratio(1, 0)
+        detect(3, 0)
+        detect(3, 1)
+        copy_out(3, 0)
+        copy_out(3, 1)
         detect(5, 0)
         detect(5, 1)
-        store_pair(1, 1)
-        detect(7, 0)
-        detect(7, 1)
         copy_out(5, 2)
         copy_out(5, 3)
-        detect(4, 2)
-        detect(4, 3)
+        detect(3, 2)
+        detect(3, 3)
+        detect(4, 0)
+        detect(4, 1)
+        store_pair(3, 1)
+        ratio(6, 0)
+        ratio(7, 0)
         copy_out(5, 0)
         copy_out(5, 1)
-        copy_out(7, 0)
-        copy_out(7, 1)
-        detect(6, 0)
-        detect(6, 1)
-        store_pair(1, 3)
+        store_pair(5, 3)
+        copy_out(3, 2)
+        copy_out(3, 3)
+        copy_out(4, 0)
+        copy_out(4, 1)
+        detect(2, 0)
+        detect(2, 1)
+        ratio(6, 1)
+        ratio(7, 1)
+        detect(2, 2)
+        detect(2, 3)
+        store_pair(5, 1)
+        copy_out(2, 0)
+        copy_out(2, 1)
+        turn_r(0, 0)
+        turn_r(1, 0)
+        copy_out(2, 2)
+        copy_out(2, 3)
+        group_r(0, 0)
+        group_r(1, 0)
+        store_pair(3, 3)
+        turn_r(6, 0)
+        turn_r(7, 0)
+        detect(4, 2)
+        detect(4, 3)
+        store_pair(4, 1)
+        store_pair(2, 3)
+        group_r(6, 0)
+        group_r(7, 0)
+        quantise_r(0, 0)
+        quantise_r(1, 0)
+        detect(0, 0)
+        detect(0, 1)
+        store_pair(2, 1)
         copy_out(4, 2)
         copy_out(4, 3)
+        copy_out(0, 0)
+        copy_out(0, 1)
+        quantise_r(6, 0)
+        quantise_r(7, 0)
+        detect(0, 2)
+        detect(0, 3)
+        copy_out(0, 2)
+        copy_out(0, 3)
+        detect(1, 0)
+        detect(1, 1)
+        detect(1, 2)
+        detect(1, 3)
+        store_pair(4, 3)
+        detect(7, 0)
+        detect(7, 1)
+        store_pair(0, 1)
+        copy_out(1, 0)
+        copy_out(1, 1)
+        store_pair(0, 3)
+        copy_out(1, 2)
+        copy_out(1, 3)
+        detect(6, 0)
+        detect(6, 1)
+        store_pair(1, 1)
+        copy_out(7, 0)
         copy_out(6, 0)
-        copy_out(6, 1)
         detect(6, 2)
         detect(6, 3)
+        copy_out(6, 3)
+        store_pair(1, 3)
         detect(7, 2)
         detect(7, 3)
-        store_pair(4, 1)
-        store_pair(5, 3)
-        store_pair(5, 1)
-        copy_out(6, 2)
-        copy_out(6, 3)
-        store_one(7, 0)
-        last_bank(0, 0)
+        copy_out(7, 1)
         store_one(7, 1)
-        store_pair(4, 3)
+        store_one(7, 0)
+        copy_out(6, 1)
+        copy_out(6, 2)
+        store_one(6, 0)
+        store_one(6, 1)
         last_bank(1, 0)
-        store_pair(6, 1)
-        store_pair(6, 3)
-        last_store(1, 0)
-        last_store(0, 0)
+        store_one(6, 3)
+        last_bank(0, 0)
+        store_one(6, 2)
         copy_out(7, 2)
+        last_store(0, 0)
+        last_store(1, 0)
         store_one(7, 2)

@@ -117,12 +117,12 @@ def tile_bearing_time_normaliser_s3_kernel(tc, x, a_words, a_scales, c, y, e, w_
 
         scalar_copy, vector_copy = nc.scalar.copy, nc.vector.tensor_copy
         copy_for = {
-            "words_x": lambda i: vector_copy,
-            "words_c": lambda i: vector_copy if i < 2 else scalar_copy,
+            "words_x": lambda i: vector_copy if i < 5 else scalar_copy,
+            "words_c": lambda i: vector_copy if i < 3 else scalar_copy,
             "group_x": lambda i: scalar_copy,
-            "group_c": lambda i: scalar_copy,
+            "group_c": lambda i: vector_copy,
             "group_r": lambda i: (vector_copy, scalar_copy)[i % 2],
-            "copy_out": lambda n: (vector_copy, scalar_copy, scalar_copy, vector_copy)[n],
+            "copy_out": lambda n: (scalar_copy, scalar_copy, vector_copy, scalar_copy)[n],
         }
 
         def words_x(i, n):
@@ -251,270 +251,270 @@ def tile_bearing_time_normaliser_s3_kernel(tc, x, a_words, a_scales, c, y, e, w_
         nc.scalar.activation(out=warm_out[:], in_=warm_in[:], func=EXP, scale=-1.0)
 
         load_rows(c, c_raw, "c_raw", 0, 4)
-        load_rows(c, c_raw, "c_raw", 4, 8)
+        load_rows(x, x_raw, "x_raw", 0, 2)
+        load_rows(x, x_raw, "x_raw", 6, 8)
         load_rows(x, x_raw, "x_raw", 2, 4)
-        load_rows(x, x_raw, "x_raw", 4, 6)
         load_scales(a_sc, a_scales)
         nc.sync.dma_start(out=a_sb[:].bitcast(I32), in_=a_words.rearrange("g p n -> p g n").bitcast(I32))
         nc.sync.dma_start(out=y_raw[:], in_=y.rearrange("(p t) n -> p t n", t=4))
-        load_rows(x, x_raw, "x_raw", 0, 2)
+        load_rows(x, x_raw, "x_raw", 4, 6)
+        load_rows(c, c_raw, "c_raw", 4, 8)
         load_rows(e, e_raw, "e_raw", 0, 2)
         load_rows(e, e_raw, "e_raw", 4, 6)
-        load_rows(x, x_raw, "x_raw", 6, 8)
-        load_rows(e, e_raw, "e_raw", 6, 8)
         load_rows(e, e_raw, "e_raw", 2, 4)
         load_w(1)
         load_scales(w_sc, w_scales)
         load_w(0)
-        warm_up(4, 0)
+        load_rows(e, e_raw, "e_raw", 6, 8)
+        warm_up(1, 0)
+        warm_up(5, 0)
+        warm_up(2, 0)
         words_c(2, 0)
         words_c(3, 0)
-        words_c(6, 0)
-        words_c(7, 0)
-        warm_up(1, 0)
-        warm_up(7, 0)
-        warm_up(5, 0)
-        turn_c(2, 0)
-        turn_c(3, 0)
-        warm_up(3, 0)
-        warm_up(6, 0)
-        group_c(2, 0)
-        group_c(3, 0)
-        turn_c(6, 0)
-        turn_c(7, 0)
         words_c(0, 0)
         words_c(1, 0)
-        words_x(2, 0)
-        words_x(3, 0)
-        words_x(4, 0)
-        words_x(5, 0)
-        warm_up(0, 0)
-        warm_up(2, 0)
-        turn_x(2, 0)
-        turn_x(3, 0)
-        quantise_c(2, 0)
-        quantise_c(3, 0)
-        words_c(4, 0)
-        words_c(5, 0)
-        group_c(6, 0)
-        group_c(7, 0)
-        turn_x(4, 0)
-        turn_x(5, 0)
-        turn_c(4, 0)
-        turn_c(5, 0)
-        group_x(2, 0)
-        group_x(3, 0)
-        group_x(4, 0)
-        group_x(5, 0)
-        group_c(4, 0)
-        group_c(5, 0)
-        quantise_c(6, 0)
-        quantise_c(7, 0)
-        y_scalar(0, 0)
-        turn_c(0, 0)
-        turn_c(1, 0)
-        quantise_x(2, 0)
-        quantise_x(3, 0)
-        quantise_x(4, 0)
-        quantise_x(5, 0)
-        y_scalar(1, 0)
-        y_vector(0, 0)
-        group_c(0, 0)
-        group_c(1, 0)
-        quantise_y(0, 0)
-        across(2, 0)
-        across(3, 0)
-        across(4, 0)
-        across(5, 0)
         words_x(0, 0)
         words_x(1, 0)
-        across(2, 1)
-        across(3, 1)
-        y_vector(1, 0)
-        along(2, 0)
-        along(3, 0)
-        inverse(2, 0)
-        inverse(3, 0)
-        quantise_c(4, 0)
-        quantise_c(5, 0)
+        warm_up(0, 0)
+        turn_c(0, 0)
+        turn_c(1, 0)
+        warm_up(4, 0)
+        warm_up(6, 0)
+        turn_c(2, 0)
+        turn_c(3, 0)
         turn_x(0, 0)
         turn_x(1, 0)
-        group_x(0, 0)
-        group_x(1, 0)
-        across(4, 1)
-        across(5, 1)
-        quantise_y(1, 0)
-        along(4, 0)
-        along(5, 0)
-        along(4, 1)
-        along(5, 1)
-        along(2, 1)
-        along(3, 1)
-        inverse(4, 0)
-        inverse(5, 0)
-        inverse(2, 1)
-        inverse(3, 1)
-        quantise_c(0, 0)
-        quantise_c(1, 0)
-        quantise_x(0, 0)
-        quantise_x(1, 0)
-        across(0, 0)
-        across(1, 0)
-        along(0, 0)
-        along(1, 0)
+        group_c(0, 0)
+        group_c(1, 0)
+        warm_up(7, 0)
         words_x(6, 0)
         words_x(7, 0)
-        ratio(4, 0)
-        ratio(5, 0)
-        ratio(2, 0)
-        ratio(3, 0)
+        group_x(0, 0)
+        group_x(1, 0)
+        words_x(2, 0)
+        words_x(3, 0)
+        group_c(2, 0)
+        group_c(3, 0)
+        warm_up(3, 0)
+        quantise_x(0, 0)
+        quantise_x(1, 0)
+        turn_x(2, 0)
+        turn_x(3, 0)
+        group_x(2, 0)
+        group_x(3, 0)
         turn_x(6, 0)
         turn_x(7, 0)
-        inverse(4, 1)
-        inverse(5, 1)
-        across(0, 1)
-        across(1, 1)
-        along(0, 1)
-        along(1, 1)
-        ratio(2, 1)
-        ratio(3, 1)
-        ratio(4, 1)
-        ratio(5, 1)
         group_x(6, 0)
         group_x(7, 0)
-        turn_r(2, 0)
-        turn_r(3, 0)
-        inverse(0, 0)
-        inverse(1, 0)
-        inverse(0, 1)
-        inverse(1, 1)
-        turn_r(4, 0)
-        turn_r(5, 0)
+        quantise_c(0, 0)
+        quantise_c(1, 0)
+        quantise_x(2, 0)
+        quantise_x(3, 0)
+        y_scalar(0, 0)
+        across(0, 0)
+        across(1, 0)
+        quantise_c(2, 0)
+        quantise_c(3, 0)
+        y_vector(0, 0)
+        across(2, 1)
+        across(3, 1)
+        across(0, 1)
+        across(1, 1)
+        y_scalar(1, 0)
+        y_vector(1, 0)
+        quantise_y(0, 0)
+        quantise_y(1, 0)
+        across(2, 0)
+        across(3, 0)
+        along(0, 0)
+        along(1, 0)
+        along(2, 0)
+        along(3, 0)
+        words_x(4, 0)
+        words_x(5, 0)
+        along(2, 1)
+        along(3, 1)
+        words_c(6, 0)
+        words_c(7, 0)
         quantise_x(6, 0)
         quantise_x(7, 0)
-        group_r(4, 0)
-        group_r(5, 0)
-        group_r(2, 0)
-        group_r(3, 0)
-        across(6, 0)
-        across(7, 0)
-        quantise_r(4, 0)
-        quantise_r(5, 0)
-        along(6, 0)
-        along(7, 0)
-        across(6, 1)
-        across(7, 1)
-        quantise_r(2, 0)
-        quantise_r(3, 0)
-        along(6, 1)
-        along(7, 1)
-        detect(5, 2)
-        detect(5, 3)
-        ratio(0, 1)
-        ratio(1, 1)
-        inverse(6, 1)
-        inverse(7, 1)
-        inverse(6, 0)
-        inverse(7, 0)
+        inverse(0, 0)
+        inverse(1, 0)
+        turn_c(6, 0)
+        turn_c(7, 0)
         ratio(0, 0)
         ratio(1, 0)
-        detect(3, 0)
-        detect(3, 1)
-        copy_out(3, 0)
-        copy_out(3, 1)
-        detect(5, 0)
-        detect(5, 1)
-        copy_out(5, 2)
-        copy_out(5, 3)
-        detect(3, 2)
-        detect(3, 3)
-        detect(4, 0)
-        detect(4, 1)
-        store_pair(3, 1)
-        ratio(6, 0)
-        ratio(7, 0)
-        copy_out(5, 0)
-        copy_out(5, 1)
-        store_pair(5, 3)
-        copy_out(3, 2)
-        copy_out(3, 3)
-        copy_out(4, 0)
-        copy_out(4, 1)
-        detect(2, 0)
-        detect(2, 1)
-        ratio(6, 1)
-        ratio(7, 1)
-        detect(2, 2)
-        detect(2, 3)
-        store_pair(5, 1)
-        copy_out(2, 0)
-        copy_out(2, 1)
+        group_c(6, 0)
+        group_c(7, 0)
+        inverse(2, 1)
+        inverse(3, 1)
+        along(0, 1)
+        along(1, 1)
+        quantise_c(6, 0)
+        quantise_c(7, 0)
+        across(6, 0)
+        across(7, 0)
+        inverse(0, 1)
+        inverse(1, 1)
+        inverse(2, 0)
+        inverse(3, 0)
+        along(6, 0)
+        along(7, 0)
+        ratio(0, 1)
+        ratio(1, 1)
+        turn_x(4, 0)
+        turn_x(5, 0)
+        inverse(6, 0)
+        inverse(7, 0)
         turn_r(0, 0)
         turn_r(1, 0)
-        copy_out(2, 2)
-        copy_out(2, 3)
+        across(6, 1)
+        across(7, 1)
         group_r(0, 0)
         group_r(1, 0)
-        store_pair(3, 3)
-        turn_r(6, 0)
-        turn_r(7, 0)
-        detect(4, 2)
-        detect(4, 3)
-        store_pair(4, 1)
-        store_pair(2, 3)
-        group_r(6, 0)
-        group_r(7, 0)
+        along(6, 1)
+        along(7, 1)
+        words_c(4, 0)
+        words_c(5, 0)
         quantise_r(0, 0)
         quantise_r(1, 0)
         detect(0, 0)
         detect(0, 1)
-        store_pair(2, 1)
-        copy_out(4, 2)
-        copy_out(4, 3)
-        copy_out(0, 0)
-        copy_out(0, 1)
-        quantise_r(6, 0)
-        quantise_r(7, 0)
-        detect(0, 2)
-        detect(0, 3)
-        copy_out(0, 2)
-        copy_out(0, 3)
-        detect(1, 0)
-        detect(1, 1)
+        group_x(4, 0)
+        group_x(5, 0)
         detect(1, 2)
         detect(1, 3)
-        store_pair(4, 3)
-        detect(7, 0)
-        detect(7, 1)
+        ratio(2, 1)
+        ratio(3, 1)
+        detect(0, 2)
+        detect(0, 3)
+        ratio(2, 0)
+        ratio(3, 0)
+        inverse(6, 1)
+        inverse(7, 1)
+        copy_out(0, 0)
+        copy_out(0, 1)
+        turn_r(2, 0)
+        turn_r(3, 0)
+        quantise_x(4, 0)
+        quantise_x(5, 0)
+        turn_c(4, 0)
+        turn_c(5, 0)
+        copy_out(1, 2)
+        copy_out(1, 3)
+        detect(1, 0)
+        detect(1, 1)
+        copy_out(0, 2)
+        copy_out(0, 3)
+        group_c(4, 0)
+        group_c(5, 0)
+        group_r(2, 0)
+        group_r(3, 0)
+        across(4, 0)
+        across(5, 0)
+        quantise_c(4, 0)
+        quantise_c(5, 0)
+        quantise_r(2, 0)
+        quantise_r(3, 0)
         store_pair(0, 1)
         copy_out(1, 0)
         copy_out(1, 1)
+        along(4, 0)
+        along(5, 0)
+        ratio(6, 1)
+        ratio(7, 1)
+        across(4, 1)
+        across(5, 1)
         store_pair(0, 3)
-        copy_out(1, 2)
-        copy_out(1, 3)
-        detect(6, 0)
-        detect(6, 1)
+        along(4, 1)
+        along(5, 1)
+        store_pair(1, 3)
+        inverse(4, 0)
+        inverse(5, 0)
+        detect(2, 0)
+        detect(2, 1)
+        copy_out(2, 0)
+        copy_out(2, 1)
+        ratio(6, 0)
+        ratio(7, 0)
+        inverse(4, 1)
+        inverse(5, 1)
+        detect(2, 2)
+        detect(2, 3)
         store_pair(1, 1)
-        copy_out(7, 0)
-        copy_out(6, 0)
+        store_pair(2, 1)
+        copy_out(2, 2)
+        copy_out(2, 3)
+        store_pair(2, 3)
+        turn_r(6, 0)
+        turn_r(7, 0)
+        detect(3, 2)
+        detect(3, 3)
+        detect(3, 0)
+        detect(3, 1)
+        group_r(6, 0)
+        group_r(7, 0)
+        copy_out(3, 2)
+        copy_out(3, 3)
+        copy_out(3, 0)
+        copy_out(3, 1)
+        store_pair(3, 3)
+        quantise_r(6, 0)
+        quantise_r(7, 0)
         detect(6, 2)
         detect(6, 3)
+        ratio(4, 0)
+        ratio(5, 0)
+        ratio(4, 1)
+        ratio(5, 1)
+        detect(6, 0)
+        detect(6, 1)
         copy_out(6, 3)
-        store_pair(1, 3)
+        copy_out(6, 0)
+        copy_out(6, 2)
+        store_pair(3, 1)
+        store_one(6, 0)
+        turn_r(4, 0)
+        turn_r(5, 0)
+        copy_out(6, 1)
+        detect(7, 0)
+        detect(7, 1)
+        group_r(4, 0)
+        group_r(5, 0)
+        copy_out(7, 0)
+        copy_out(7, 1)
+        quantise_r(4, 0)
+        quantise_r(5, 0)
+        store_one(6, 2)
+        store_one(6, 3)
+        detect(4, 0)
+        detect(4, 1)
+        store_one(6, 1)
+        store_one(7, 1)
+        detect(5, 0)
+        detect(5, 1)
+        store_one(7, 0)
+        copy_out(4, 0)
+        copy_out(4, 1)
+        copy_out(5, 0)
+        copy_out(5, 1)
+        detect(5, 2)
+        detect(5, 3)
+        copy_out(5, 2)
+        copy_out(5, 3)
+        detect(4, 2)
+        detect(4, 3)
+        store_pair(4, 1)
+        store_pair(5, 1)
+        store_pair(5, 3)
+        copy_out(4, 2)
+        copy_out(4, 3)
+        store_pair(4, 3)
         detect(7, 2)
         detect(7, 3)
-        copy_out(7, 1)
-        store_one(7, 1)
-        store_one(7, 0)
-        copy_out(6, 1)
-        copy_out(6, 2)
-        store_one(6, 0)
-        store_one(6, 1)
-        last_bank(1, 0)
-        store_one(6, 3)
-        last_bank(0, 0)
-        store_one(6, 2)
         copy_out(7, 2)
+        last_bank(0, 0)
         last_store(0, 0)
-        last_store(1, 0)
         store_one(7, 2)
+        last_bank(1, 0)
+        last_store(1, 0)

from contextlib import ExitStack

import concourse.mybir as mybir
from concourse.masks import make_identity

FLOPS = 2 * 1024 * 1024 * 1024 + 2 * 1024 * 512 * 1024 + 2 * 1024 * 1024 * 2048

F32 = mybir.dt.float32
BF16 = mybir.dt.bfloat16
I32 = mybir.dt.int32
U32 = mybir.dt.uint32
U8 = mybir.dt.uint8
FP8X4 = mybir.dt.float8_e4m3fn_x4
FP4X4 = mybir.dt.float4_e2m1fn_x4
EXP = mybir.ActivationFunctionType.Exp
MULT = mybir.AluOpType.mult

P = 128
TILES = 8
B, H, D = 1024, 512, 2048
G = B // 512
NB = 512
BANKS = 8
Y_V = 352


def tile_bearing_time_normaliser_s3_kernel(tc, x, a_words, a_scales, c, y, e, w_words, w_scales, out):
    nc = tc.nc
    with ExitStack() as ctx:
        keep = ctx.enter_context(tc.tile_pool(name="keep", bufs=1))
        work = ctx.enter_context(tc.tile_pool(name="work", bufs=5))
        psum = ctx.enter_context(tc.psum_pool(name="psum", bufs=BANKS))
        ctx.enter_context(tc.manual_schedule())

        ident = keep.tile([P, P], F32)
        a_sb = keep.tile([P, G, 2 * B], U8, align_bytes=64)
        a_sc = keep.tile([P, G, B], U8, align_bytes=64)
        w_sb = [keep.tile([P, G, D], U8, tag="w_sb", name="w_sb", bufs=2, align_bytes=64) for h in range(2)]
        w_sc = keep.tile([P, G, D], U8, align_bytes=64)
        y_raw = keep.tile([P, 4, B], BF16)
        y_codes = keep.tile([P, B], U32, align_bytes=64)
        y_sc = keep.tile([P, B], U8, align_bytes=64)
        warm_in = keep.tile([P, 8], F32)
        warm_out = keep.tile([P, 8], F32)

        x_raw, c_raw, e_raw = {}, {}, {}
        x_words, c_words, r_words = {}, {}, {}
        x_ps, c_ps, r_ps, l_ps, o_ps = {}, {}, {}, {}, {}
        x_grp, c_grp, r_grp, y_grp = {}, {}, {}, {}
        x_q, c_q, r_q = {}, {}, {}
        inv_bg, o_sb = {}, {}

        out_rows = out.rearrange("(p i) d -> p i d", i=TILES)

        def load_rows(src, raw, tag, lo, hi):
            rows = src.rearrange("(p i) b -> p i b", i=TILES)
            t = keep.tile([P, hi - lo, rows.shape[2]], BF16, tag=tag + str(lo), name=tag + str(lo))
            nc.sync.dma_start(out=t[:], in_=rows[:, lo:hi, :])
            for i in range(lo, hi):
                raw[i] = t[:, i - lo, :]

        def load_scales(dst, src):
            for q in range(4):
                nc.sync.dma_start(
                    out=dst[32 * q:32 * q + 4, :, :].bitcast(I32),
                    in_=src[:, 4 * q:4 * q + 4, :].rearrange("g r n -> r g n").bitcast(I32),
                )

        def load_w(h):
            nc.sync.dma_start(
                out=w_sb[h][:].bitcast(I32),
                in_=w_words[:, :, h * D:(h + 1) * D].rearrange("g p n -> p g n").bitcast(I32))

        def order_words(copy, raw, passes, tag):
            t = work.tile([P, passes * 256], F32, tag=tag, name=tag)
            copy(
                out=t[:].rearrange("p (g u m) -> p g u m", g=passes, u=2),
                in_=raw.bitcast(F32).rearrange("p (g m u) -> p g u m", g=passes, u=2),
            )
            return t

        def new_bank():
            t = psum.tile([P, NB], F32, tag="bank", name="bank")
            return t

        def transpose_words(words, count):
            t = new_bank()
            for j in range(count):
                nc.tensor.transpose(t[:, j * P:(j + 1) * P], words[:, j * P:(j + 1) * P], ident[:])
            return t

        def interleave(copy, bank, passes, tag):
            t = work.tile([P, passes, P, 4], BF16, tag=tag, name=tag, align_bytes=64)
            copy(
                out=t[:].rearrange("p g r t -> p (g r t)").bitcast(F32).rearrange("p (g r u) -> p g r u", g=passes, u=2),
                in_=bank[:, :passes * 2 * P].rearrange("p (g u r) -> p g r u", g=passes, u=2),
            )
            return t

        def quantise(grp, passes, tag):
            codes = work.tile([P, passes * P], U32, tag=tag + "_codes", name=tag + "_codes", bufs=TILES, align_bytes=64)
            scales = work.tile([P, passes * P], U8, tag=tag + "_sc", name=tag + "_sc", bufs=TILES, align_bytes=64)
            nc.vector.quantize_mx(
                out=codes[:].bitcast(FP8X4), scales=scales[:], in_=grp[:].rearrange("p g r t -> p (g r t)"))
            return codes, scales

        def mx_pass(bank, operand, g, codes, code_type, scales, start, stop):
            nc.tensor.matmul_mx(
                out=bank[:],
                lhsT=operand[0][:, g * P:(g + 1) * P].bitcast(FP8X4),
                lhsT_scale=operand[1][:, g * P:(g + 1) * P],
                rhs=codes.bitcast(code_type),
                rhs_scale=scales,
                start=start,
                stop=stop,
            )

        scalar_copy, vector_copy = nc.scalar.copy, nc.vector.tensor_copy
        copy_for = {
            "words_x": lambda i: vector_copy if i < 5 else scalar_copy,
            "words_c": lambda i: vector_copy if i < 3 else scalar_copy,
            "group_x": lambda i: scalar_copy,
            "group_c": lambda i: vector_copy,
            "group_r": lambda i: (vector_copy, scalar_copy)[i % 2],
            "copy_out": lambda n: (scalar_copy, scalar_copy, vector_copy, scalar_copy)[n],
        }

        def words_x(i, n):
            x_words[i] = order_words(copy_for["words_x"](i), x_raw[i], G, "x_words")

        def words_c(i, n):
            c_words[i] = order_words(copy_for["words_c"](i), c_raw[i], 1, "c_words")

        def turn_x(i, n):
            x_ps[i] = transpose_words(x_words[i], 4)

        def turn_c(i, n):
            c_ps[i] = transpose_words(c_words[i], 2)

        def group_x(i, n):
            x_grp[i] = interleave(copy_for["group_x"](i), x_ps[i], G, "x_grp")

        def group_c(i, n):
            c_grp[i] = interleave(copy_for["group_c"](i), c_ps[i], 1, "c_grp")

        def quantise_x(i, n):
            x_q[i] = quantise(x_grp[i], G, "x")

        def quantise_c(i, n):
            c_q[i] = quantise(c_grp[i], 1, "c")

        def y_group(h):
            if h not in y_grp:
                t = keep.tile([P, NB, 4], BF16, tag="y_grp", name="y_grp", bufs=2, align_bytes=64)
                y_grp[h] = t
            return y_grp[h]

        def y_vector(h, n):
            lo = h * NB
            nc.vector.tensor_copy(out=y_group(h)[:, :Y_V, :], in_=y_raw[:, :, lo:lo + Y_V].rearrange("p t n -> p n t"))

        def y_scalar(h, n):
            lo, hi = h * NB + Y_V, (h + 1) * NB
            nc.scalar.copy(out=y_group(h)[:, Y_V:, :], in_=y_raw[:, :, lo:hi].rearrange("p t n -> p n t"))

        def quantise_y(h, n):
            cols = slice(h * NB, (h + 1) * NB)
            nc.vector.quantize_mx(
                out=y_codes[:, cols].bitcast(FP8X4), scales=y_sc[:, cols], in_=y_grp[h][:].rearrange("p n t -> p (n t)"))

        def across(i, n):
            l_ps[i, n] = new_bank()
            for g in range(G):
                mx_pass(l_ps[i, n], x_q[i], g, a_sb[:, g, 2 * NB * n:2 * NB * (n + 1)], FP4X4,
                        a_sc[:, g, NB * n:NB * (n + 1)], start=(g == 0), stop=False)

        def along(i, n):
            cols = slice(NB * n, NB * (n + 1))
            mx_pass(l_ps[i, n], c_q[i], 0, y_codes[:, cols], FP8X4, y_sc[:, cols], start=False, stop=True)

        def inverse(i, n):
            t = work.tile([P, NB], F32, tag="inv_bg", name="inv_bg", bufs=8)
            nc.scalar.activation(out=t[:], in_=l_ps[i, n][:], func=EXP, scale=-1.0)
            inv_bg[i, n] = t

        def ratio(i, n):
            if i not in r_words:
                t = work.tile([P, B], BF16, tag="r_words", name="r_words", bufs=6)
                r_words[i] = t
            cols = slice(n * NB, (n + 1) * NB)
            nc.vector.tensor_tensor(
                out=r_words[i][:, cols].rearrange("p (u m h) -> p u m h", u=2, h=2),
                in0=inv_bg[i, n][:].rearrange("p (m u h) -> p u m h", u=2, h=2),
                in1=e_raw[i][:, cols].rearrange("p (m u h) -> p u m h", u=2, h=2),
                op=MULT,
            )

        def turn_r(i, n):
            r_ps[i] = transpose_words(r_words[i][:].bitcast(F32), 4)

        def group_r(i, n):
            r_grp[i] = interleave(copy_for["group_r"](i), r_ps[i], G, "r_grp")

        def quantise_r(i, n):
            r_q[i] = quantise(r_grp[i], G, "r")

        def detect(i, n):
            o_ps[i, n] = new_bank()
            for g in range(G):
                mx_pass(o_ps[i, n], r_q[i], g, w_sb[n // 2][:, g, 2 * NB * (n % 2):2 * NB * (n % 2 + 1)], FP4X4,
                        w_sc[:, g, NB * n:NB * (n + 1)], start=(g == 0), stop=(g == G - 1))

        def store(i, lo, hi):
            nc.sync.dma_start(out=out_rows[:, i, lo:hi], in_=o_sb[i][:, lo:hi])

        def copy_out(i, n):
            if i not in o_sb:
                t = work.tile([P, D], F32, tag="o_sb", name="o_sb", bufs=4)
                o_sb[i] = t
            if (i, n) == (TILES - 1, 3):
                return
            copy_for["copy_out"](n)(out=o_sb[i][:, n * NB:(n + 1) * NB], in_=o_ps[i, n][:])

        def store_pair(i, n):
            store(i, (n - 1) * NB, (n + 1) * NB)

        def store_one(i, n):
            store(i, n * NB, (n + 1) * NB)

        def last_bank(h, n):
            lo = 3 * NB + h * (NB // 2)
            copy = (scalar_copy, vector_copy)[h]
            copy(out=o_sb[TILES - 1][:, lo:lo + NB // 2], in_=o_ps[TILES - 1, 3][:, h * (NB // 2):(h + 1) * (NB // 2)])

        def last_store(h, n):
            lo = 3 * NB + h * (NB // 2)
            store(TILES - 1, lo, lo + NB // 2)

        def warm_up(j, n):
            bank = new_bank()
            nc.tensor.matmul_mx(
                out=bank[:], lhsT=y_codes[:, :P].bitcast(FP8X4), lhsT_scale=y_sc[:, :P],
                rhs=y_codes[:, :NB].bitcast(FP8X4), rhs_scale=y_sc[:, :NB], start=True, stop=True)

        nc.vector.memset(y_codes[:, :NB].bitcast(I32), 0)
        nc.vector.memset(y_sc[:, :NB].bitcast(I32), 0)
        nc.vector.memset(warm_in[:], 0.0)
        nc.vector.memset(a_sc[:].rearrange("p g n -> p (g n)").bitcast(I32), 0)
        nc.vector.memset(w_sc[:].rearrange("p g n -> p (g n)").bitcast(I32), 0)
        make_identity(nc, ident[:])
        nc.scalar.activation(out=warm_out[:], in_=warm_in[:], func=EXP, scale=-1.0)

        load_rows(c, c_raw, "c_raw", 0, 4)
        load_rows(x, x_raw, "x_raw", 0, 2)
        load_rows(x, x_raw, "x_raw", 6, 8)
        load_rows(x, x_raw, "x_raw", 2, 4)
        load_scales(a_sc, a_scales)
        nc.sync.dma_start(out=a_sb[:].bitcast(I32), in_=a_words.rearrange("g p n -> p g n").bitcast(I32))
        nc.sync.dma_start(out=y_raw[:], in_=y.rearrange("(p t) n -> p t n", t=4))
        load_rows(x, x_raw, "x_raw", 4, 6)
        load_rows(c, c_raw, "c_raw", 4, 8)
        load_rows(e, e_raw, "e_raw", 0, 2)
        load_rows(e, e_raw, "e_raw", 4, 6)
        load_rows(e, e_raw, "e_raw", 2, 4)
        load_w(1)
        load_scales(w_sc, w_scales)
        load_w(0)
        load_rows(e, e_raw, "e_raw", 6, 8)
        warm_up(1, 0)
        warm_up(5, 0)
        warm_up(2, 0)
        words_c(2, 0)
        words_c(3, 0)
        words_c(0, 0)
        words_c(1, 0)
        words_x(0, 0)
        words_x(1, 0)
        warm_up(0, 0)
        turn_c(0, 0)
        turn_c(1, 0)
        warm_up(4, 0)
        warm_up(6, 0)
        turn_c(2, 0)
        turn_c(3, 0)
        turn_x(0, 0)
        turn_x(1, 0)
        group_c(0, 0)
        group_c(1, 0)
        warm_up(7, 0)
        words_x(6, 0)
        words_x(7, 0)
        group_x(0, 0)
        group_x(1, 0)
        words_x(2, 0)
        words_x(3, 0)
        group_c(2, 0)
        group_c(3, 0)
        warm_up(3, 0)
        quantise_x(0, 0)
        quantise_x(1, 0)
        turn_x(2, 0)
        turn_x(3, 0)
        group_x(2, 0)
        group_x(3, 0)
        turn_x(6, 0)
        turn_x(7, 0)
        group_x(6, 0)
        group_x(7, 0)
        quantise_c(0, 0)
        quantise_c(1, 0)
        quantise_x(2, 0)
        quantise_x(3, 0)
        y_scalar(0, 0)
        across(0, 0)
        across(1, 0)
        quantise_c(2, 0)
        quantise_c(3, 0)
        y_vector(0, 0)
        across(2, 1)
        across(3, 1)
        across(0, 1)
        across(1, 1)
        y_scalar(1, 0)
        y_vector(1, 0)
        quantise_y(0, 0)
        quantise_y(1, 0)
        across(2, 0)
        across(3, 0)
        along(0, 0)
        along(1, 0)
        along(2, 0)
        along(3, 0)
        words_x(4, 0)
        words_x(5, 0)
        along(2, 1)
        along(3, 1)
        words_c(6, 0)
        words_c(7, 0)
        quantise_x(6, 0)
        quantise_x(7, 0)
        inverse(0, 0)
        inverse(1, 0)
        turn_c(6, 0)
        turn_c(7, 0)
        ratio(0, 0)
        ratio(1, 0)
        group_c(6, 0)
        group_c(7, 0)
        inverse(2, 1)
        inverse(3, 1)
        along(0, 1)
        along(1, 1)
        quantise_c(6, 0)
        quantise_c(7, 0)
        across(6, 0)
        across(7, 0)
        inverse(0, 1)
        inverse(1, 1)
        inverse(2, 0)
        inverse(3, 0)
        along(6, 0)
        along(7, 0)
        ratio(0, 1)
        ratio(1, 1)
        turn_x(4, 0)
        turn_x(5, 0)
        inverse(6, 0)
        inverse(7, 0)
        turn_r(0, 0)
        turn_r(1, 0)
        across(6, 1)
        across(7, 1)
        group_r(0, 0)
        group_r(1, 0)
        along(6, 1)
        along(7, 1)
        words_c(4, 0)
        words_c(5, 0)
        quantise_r(0, 0)
        quantise_r(1, 0)
        detect(0, 0)
        detect(0, 1)
        group_x(4, 0)
        group_x(5, 0)
        detect(1, 2)
        detect(1, 3)
        ratio(2, 1)
        ratio(3, 1)
        detect(0, 2)
        detect(0, 3)
        ratio(2, 0)
        ratio(3, 0)
        inverse(6, 1)
        inverse(7, 1)
        copy_out(0, 0)
        copy_out(0, 1)
        turn_r(2, 0)
        turn_r(3, 0)
        quantise_x(4, 0)
        quantise_x(5, 0)
        turn_c(4, 0)
        turn_c(5, 0)
        copy_out(1, 2)
        copy_out(1, 3)
        detect(1, 0)
        detect(1, 1)
        copy_out(0, 2)
        copy_out(0, 3)
        group_c(4, 0)
        group_c(5, 0)
        group_r(2, 0)
        group_r(3, 0)
        across(4, 0)
        across(5, 0)
        quantise_c(4, 0)
        quantise_c(5, 0)
        quantise_r(2, 0)
        quantise_r(3, 0)
        store_pair(0, 1)
        copy_out(1, 0)
        copy_out(1, 1)
        along(4, 0)
        along(5, 0)
        ratio(6, 1)
        ratio(7, 1)
        across(4, 1)
        across(5, 1)
        store_pair(0, 3)
        along(4, 1)
        along(5, 1)
        store_pair(1, 3)
        inverse(4, 0)
        inverse(5, 0)
        detect(2, 0)
        detect(2, 1)
        copy_out(2, 0)
        copy_out(2, 1)
        ratio(6, 0)
        ratio(7, 0)
        inverse(4, 1)
        inverse(5, 1)
        detect(2, 2)
        detect(2, 3)
        store_pair(1, 1)
        store_pair(2, 1)
        copy_out(2, 2)
        copy_out(2, 3)
        store_pair(2, 3)
        turn_r(6, 0)
        turn_r(7, 0)
        detect(3, 2)
        detect(3, 3)
        detect(3, 0)
        detect(3, 1)
        group_r(6, 0)
        group_r(7, 0)
        copy_out(3, 2)
        copy_out(3, 3)
        copy_out(3, 0)
        copy_out(3, 1)
        store_pair(3, 3)
        quantise_r(6, 0)
        quantise_r(7, 0)
        detect(6, 2)
        detect(6, 3)
        ratio(4, 0)
        ratio(5, 0)
        ratio(4, 1)
        ratio(5, 1)
        detect(6, 0)
        detect(6, 1)
        copy_out(6, 3)
        copy_out(6, 0)
        copy_out(6, 2)
        store_pair(3, 1)
        store_one(6, 0)
        turn_r(4, 0)
        turn_r(5, 0)
        copy_out(6, 1)
        detect(7, 0)
        detect(7, 1)
        group_r(4, 0)
        group_r(5, 0)
        copy_out(7, 0)
        copy_out(7, 1)
        quantise_r(4, 0)
        quantise_r(5, 0)
        store_one(6, 2)
        store_one(6, 3)
        detect(4, 0)
        detect(4, 1)
        store_one(6, 1)
        store_one(7, 1)
        detect(5, 0)
        detect(5, 1)
        store_one(7, 0)
        copy_out(4, 0)
        copy_out(4, 1)
        copy_out(5, 0)
        copy_out(5, 1)
        detect(5, 2)
        detect(5, 3)
        copy_out(5, 2)
        copy_out(5, 3)
        detect(4, 2)
        detect(4, 3)
        store_pair(4, 1)
        store_pair(5, 1)
        store_pair(5, 3)
        copy_out(4, 2)
        copy_out(4, 3)
        store_pair(4, 3)
        detect(7, 2)
        detect(7, 3)
        copy_out(7, 2)
        last_bank(0, 0)
        last_store(0, 0)
        store_one(7, 2)
        last_bank(1, 0)
        last_store(1, 0)
